import numpy as np
import ml_dtypes


def mxq(x, axis, fmt="e4m3"):
    dtype, down = {"e4m3": (ml_dtypes.float8_e4m3fn, 7), "e5m2": (ml_dtypes.float8_e5m2, 14)}[fmt]
    v = np.moveaxis(np.asarray(x, np.float32).astype(ml_dtypes.bfloat16).astype(np.float64), axis, -1)
    blocks = v.reshape(v.shape[:-1] + (-1, 32))
    amax = np.abs(blocks).max(-1, keepdims=True)
    byte = np.maximum(np.where(amax > 0, np.frexp(amax)[1] - 1 + 127, 0) - down, 1)
    scale = np.exp2(byte - 127.0)
    codes = (blocks / scale).astype(np.float32).astype(dtype).astype(np.float64)
    return np.moveaxis((codes * scale).reshape(v.shape), -1, axis)


WIDE = False


def mx_kscale(k):
    if not WIDE:
        return np.ones(k)
    levels = np.array([10, -10, 5, -5, 0])
    if k % 512:
        return np.exp2(np.random.permutation(np.resize(levels, k // 32))).repeat(32)
    a = np.empty((k // 512, 16))
    for p in range(k // 512):
        a[p, :8] = np.random.permutation(np.resize(levels, 8))
        for g in range(8):
            far = levels[np.abs(levels - a[p, g]) >= 10]
            a[p, g + 8] = far[np.random.randint(len(far))]
    return np.exp2(a.ravel()).repeat(32)


BF16 = ml_dtypes.bfloat16


def bf(x):
    return np.asarray(x, np.float32).astype(BF16)


def f64(x):
    return np.asarray(x).astype(np.float64)


B, D, P = 1024, 512, 512


def split_vkq(h, d):
    return h[:, :d], h[:, d:2 * d], h[:, 2 * d:3 * d]


def score(k, q, d):
    return np.sum(k * q, axis=-1) / np.sqrt(d)


def sigmoid(v):
    return 1.0 / (1.0 + np.exp(-v))


def draw0():
    t = mx_kscale(P)
    return {"q_prev": bf(np.random.standard_normal((B, D))),
            "wt": bf(np.random.standard_normal((D, P)) * (1.4 / np.sqrt(D)) * t),
            "bt": bf(np.random.standard_normal(P) * 0.4 * t),
            "q_cur": bf(np.random.standard_normal((B, P)) * t),
            "wvkq": bf(np.random.standard_normal((P, 3 * D)) / np.sqrt(P) / t[:, None])}


def core(q_prev, wt, bt, q_cur, wvkq):
    d = q_prev.shape[1]
    p = np.maximum(f64(q_prev) @ f64(wt) + f64(bt), 0.0)
    wq = mxq(f64(wvkq), 0, "e4m3")
    hp = mxq(p, 1, "e4m3") @ wq
    hc = mxq(f64(q_cur), 1, "e4m3") @ wq
    vp, kp, qp = split_vkq(hp, d)
    vc, kc, qc = split_vkq(hc, d)
    sp = score(kp, qp, d)
    sc = score(kc, qc, d)
    a = sigmoid(sp - sc)
    return a[:, None] * vp + (1.0 - a)[:, None] * vc


def e4m3fn_bytes(y):
    return np.clip(np.asarray(y, np.float64), -448.0, 448.0).astype(np.float32).astype(ml_dtypes.float8_e4m3fn).view(np.uint8)


def e4m3fn_values(b):
    return np.asarray(b, np.uint8).view(ml_dtypes.float8_e4m3fn).astype(np.float64)


def setup_inputs():
    d = draw0()
    x0 = np.asarray(d['wvkq']).astype(np.float64)
    s = (np.max(np.abs(x0), axis=(1,), keepdims=True) / 448.0).astype(np.float32)
    out = {}
    for k, v in d.items():
        if k == 'wvkq':
            out['wvkq_bytes'] = e4m3fn_bytes(x0 / s.astype(np.float64))
            out['wvkq_scale'] = s
        else:
            out[k] = v
    return out


def reference(q_prev, wt, bt, q_cur, wvkq_bytes, wvkq_scale):
    return core(q_prev, wt, bt, q_cur, e4m3fn_values(wvkq_bytes) * wvkq_scale.astype(np.float64))

@@ -1,0 +1,352 @@
+import math
+from contextlib import ExitStack
+
+import concourse.mybir as mybir
+from concourse.masks import make_identity
+
+B, D, C = 1024, 512, 512
+FLOPS = 2 * B * D * C + 2 * 2 * B * C * 3 * D
+
+F32 = mybir.dt.float32
+BF16 = mybir.dt.bfloat16
+U32 = mybir.dt.uint32
+U8 = mybir.dt.uint8
+FP8 = mybir.dt.float8_e4m3fn
+FP8X4 = mybir.dt.float8_e4m3fn_x4
+ACT = mybir.ActivationFunctionType
+ALU = mybir.AluOpType
+
+P = 128
+PACK = 4
+HALF = 512
+V_COLS, K_COLS, Q_COLS = 0, 1, 2
+WARM_UP_MATMULS = 6
+
+
+def tile_aitmadaptiveinfotransfer_kernel(tc, q_prev, wt, bt, q_cur, wvkq_bytes, wvkq_scale, out):
+    nc = tc.nc
+    with ExitStack() as ctx:
+        keep = ctx.enter_context(tc.tile_pool(name="keep", bufs=1))
+        work = ctx.enter_context(tc.tile_pool(name="work", bufs=4))
+        psum = ctx.enter_context(tc.psum_pool(name="psum", bufs=8))
+        ctx.enter_context(tc.manual_schedule())
+
+        def bank(name):
+            return psum.tile([P, 512], F32, name=name, tag="bank")
+
+        def load(name, source, dtype, queue=nc.sync):
+            tile = keep.tile(list(source.shape), dtype, name=name, align_bytes=64)
+            queue.dma_start(out=tile[:], in_=source)
+            return tile
+
+        prev_rows = q_prev.rearrange("(h p r) d -> h p (r d)", h=2, r=PACK)
+        cur_rows = q_cur.rearrange("(h p r) d -> h p (r d)", h=2, r=PACK)
+        out_rows = out.rearrange("(h p r) n -> h r p n", h=2, r=PACK)
+        wt_rows = wt.rearrange("(u p e) c -> u p (e c)", u=2, e=2)
+        w_rows = wvkq_bytes.rearrange("(p t) n -> p t n", t=PACK)
+
+        w_scale = load("w_scale", wvkq_scale.rearrange("(p t) o -> p (t o)", t=PACK), F32, nc.scalar)
+        bias = load("bias", bt.rearrange("(p t) -> p t", t=PACK), BF16, nc.scalar)
+        prev0 = [load("prev0_%d" % i, prev_rows[0][:, 2 * D * i : 2 * D * (i + 1)], BF16) for i in range(2)]
+        wt_sb = [load("wt_0", wt_rows[0], BF16)]
+        w_bytes = {K_COLS: load("w_bytes_k", w_rows[:, :, D : 2 * D], U8)}
+        wt_sb.append(load("wt_1", wt_rows[1], BF16))
+        w_bytes[Q_COLS] = load("w_bytes_q", w_rows[:, :, 2 * D :], U8)
+        prev1 = load("prev1", prev_rows[1], BF16)
+        cur = [load("cur0", cur_rows[0], BF16)]
+        w_bytes[V_COLS] = load("w_bytes_v", w_rows[:, :, :D], U8)
+        cur.append(load("cur1", cur_rows[1], BF16))
+
+        identity = keep.tile([P, P], F32, name="identity")
+        make_identity(nc, identity[:])
+        zeros = keep.tile([P, 512], BF16, name="zeros")
+        nc.vector.memset(zeros[:], 0.0)
+        preload = keep.tile([P, 1], F32, name="preload")
+        nc.scalar.activation(out=preload[:], in_=zeros[:, 0:1], func=ACT.Sigmoid)
+        warm = bank("warm")
+        for i in range(WARM_UP_MATMULS):
+            nc.tensor.matmul(out=warm[:], lhsT=zeros[:, :P], rhs=zeros[:], start=True, stop=True)
+
+        def copy_words(engine, dst, src):
+            if engine == "vector":
+                nc.vector.tensor_copy(out=dst, in_=src)
+            else:
+                nc.scalar.copy(out=dst, in_=src)
+
+        def prev_words(h, r):
+            if h == 0:
+                return prev0[r // 2][:].bitcast(F32)[:, 256 * (r % 2) : 256 * (r % 2 + 1)]
+            return prev1[:].bitcast(F32)[:, 256 * r : 256 * (r + 1)]
+
+        def turn_prev(h):
+            banks = [bank("prev_t_%d_%d" % (h, u)) for u in range(2)]
+            for r in range(PACK):
+                for u in range(2):
+                    nc.tensor.transpose(banks[u][:, P * r : P * (r + 1)], prev_words(h, r)[:, P * u : P * (u + 1)], identity[:])
+            return banks
+
+        def empty_prev(h, u, source, engine):
+            turned = keep.tile([P, HALF], F32, name="prev_turned_%d_%d" % (h, u))
+            copy_words(engine, turned[:], source[:])
+            return turned
+
+        def turn_cur(h):
+            banks = [bank("cur_t_%d_%d" % (h, j)) for j in range(2)]
+            words = cur[h][:].bitcast(F32)
+            for r in range(PACK):
+                for u in range(2):
+                    at = 256 * (r % 2) + P * u
+                    nc.tensor.transpose(banks[r // 2][:, at : at + P], words[:, 256 * r + u : 256 * (r + 1) : 2], identity[:])
+            return banks
+
+        def empty_cur(grouped, j, source, engine):
+            dst = grouped[:].bitcast(F32)[:, HALF * j : HALF * (j + 1)]
+            copy_words(engine, dst.rearrange("p (r m u) -> p r m u", r=2, u=2), source[:].rearrange("p (r u m) -> p r m u", r=2, u=2))
+
+        def relu_layer_passes(acc, turned, t, u):
+            for e in range(2):
+                nc.tensor.matmul(
+                    out=acc[:],
+                    lhsT=wt_sb[u][:, C * e + t : C * (e + 1) : PACK],
+                    rhs=turned[u][:].bitcast(BF16)[:, e : 2 * HALF : 2],
+                    start=(u == 0 and e == 0),
+                    stop=(u == 1 and e == 1),
+                )
+
+        def relu(planes, t, acc):
+            nc.scalar.activation(out=planes[:, t, :], in_=acc[:], func=ACT.Relu, bias=bias[:, t : t + 1])
+
+        def new_planes(name):
+            return keep.tile([P, PACK, 512], BF16, name=name)
+
+        def new_grouped(name):
+            return keep.tile([P, PACK * 512], BF16, name=name, align_bytes=64)
+
+        def widen(planes, cols, t, engine):
+            source = w_bytes[cols][:, t, :].bitcast(FP8)
+            if engine == "vector":
+                nc.vector.tensor_scalar(out=planes[:, t, :], in0=source, scalar1=w_scale[:, t : t + 1], scalar2=None, op0=ALU.mult)
+            else:
+                nc.scalar.activation(out=planes[:, t, :], in_=source, func=ACT.Copy, scale=w_scale[:, t : t + 1])
+
+        def interleave(name, planes, engine):
+            grouped = new_grouped(name)
+            if engine == "vector":
+                nc.vector.tensor_copy(
+                    out=grouped[:].rearrange("p (c i t) -> p c t i", i=4, t=PACK),
+                    in_=planes[:].rearrange("p t (c i) -> p c t i", i=4),
+                )
+            else:
+                nc.gpsimd.tensor_scalar(
+                    out=grouped[:].rearrange("p (c t) -> p c t", t=PACK),
+                    in0=planes[:].rearrange("p t c -> p c t"),
+                    scalar1=1.0, scalar2=0.0, op0=ALU.mult, op1=ALU.add,
+                )
+            return grouped
+
+        def quantize(name, grouped):
+            codes = keep.tile([P, 512], U32, name=name + "_codes", align_bytes=64)
+            scales = keep.tile([P, 512], U8, name=name + "_scales", align_bytes=64)
+            nc.vector.quantize_mx(out=codes[:].bitcast(FP8X4), scales=scales[:], in_=grouped[:])
+            return codes, scales
+
+        def product(name, rows, r, weights):
+            acc = bank(name)
+            cols = slice(P * r, P * (r + 1))
+            nc.tensor.matmul_mx(
+                out=acc[:],
+                lhsT=rows[0][:, cols].bitcast(FP8X4),
+                lhsT_scale=rows[1][:, cols],
+                rhs=weights[0][:].bitcast(FP8X4),
+                rhs_scale=weights[1][:],
+                start=True,
+                stop=True,
+            )
+            return acc
+
+        tiles = 2 * PACK
+        score_prev, minus_score_cur, share_prev, share_cur = (
+            [keep.tile([P, 1], F32, name="%s_%d" % (what, i)) for i in range(tiles)]
+            for what in ("score_prev", "minus_score_cur", "share_prev", "share_cur")
+        )
+
+        def score_products(i, rows):
+            return product("k_%d" % i, rows, i % PACK, wk_q[0]), product("q_%d" % i, rows, i % PACK, wq_q[0])
+
+        def copy_keys(keys_acc):
+            keys = work.tile([P, D], F32, name="keys")
+            nc.scalar.copy(out=keys[:], in_=keys_acc[:])
+            return keys
+
+        def score(i, keys, queries, factor, result):
+            nc.vector.scalar_tensor_tensor(
+                out=keys[:], in0=queries[:], scalar=factor, in1=keys[:], op0=ALU.mult, op1=ALU.mult, accum_out=result[i][:]
+            )
+
+        def gate(i):
+            nc.scalar.activation(out=share_prev[i][:], in_=score_prev[i][:], func=ACT.Sigmoid, bias=minus_score_cur[i][:])
+            nc.gpsimd.tensor_scalar(out=share_cur[i][:], in0=share_prev[i][:], scalar1=-1.0, scalar2=1.0, op0=ALU.mult, op1=ALU.add)
+
+        def value_products(i):
+            h, r = divmod(i, PACK)
+            return product("vp_%d" % i, pq[h], r, wv_q[0]), product("vc_%d" % i, cq[h], r, wv_q[0])
+
+        def scale_prev(i, values_prev):
+            mixed = work.tile([P, D], F32, name="mixed")
+            nc.scalar.activation(out=mixed[:], in_=values_prev[:], func=ACT.Copy, scale=share_prev[i][:])
+            return mixed
+
+        def mix(i, mixed, values_cur):
+            h, r = divmod(i, PACK)
+            nc.vector.scalar_tensor_tensor(
+                out=mixed[:], in0=values_cur[:], scalar=share_cur[i][:], in1=mixed[:], op0=ALU.mult, op1=ALU.add
+            )
+            nc.sync.dma_start(out=out_rows[h][r], in_=mixed[:])
+
+        inv = 1.0 / math.sqrt(D)
+        turned = [{}, {}]
+        accs, p_grouped, w_grouped, pq, cq, B_, K_ = {}, {}, {}, {}, {}, {}, {}
+        wk_q, wq_q, wv_q = {}, {}, {}
+        w_planes = [new_planes("w_planes_%d" % c) for c in range(3)]
+        p_planes = [new_planes("p_planes_%d" % h) for h in range(2)]
+        cur_grouped = [new_grouped("cur_grouped_%d" % h) for h in range(2)]
+        B_["tp0"] = turn_prev(0)
+        turned[0][0] = empty_prev(0, 0, B_["tp0"][0], "vector")
+        turned[0][1] = empty_prev(0, 1, B_["tp0"][1], "scalar")
+        accs[0] = bank("relu0_0"); relu_layer_passes(accs[0], turned[0], 0, 0)
+        accs[1] = bank("relu0_1"); relu_layer_passes(accs[1], turned[0], 1, 0)
+        accs[2] = bank("relu0_2"); relu_layer_passes(accs[2], turned[0], 2, 0)
+        accs[3] = bank("relu0_3"); relu_layer_passes(accs[3], turned[0], 3, 0)
+        widen(w_planes[K_COLS], K_COLS, 0, "vector")
+        widen(w_planes[K_COLS], K_COLS, 1, "vector")
+        widen(w_planes[K_COLS], K_COLS, 2, "vector")
+        widen(w_planes[K_COLS], K_COLS, 3, "scalar")
+        w_grouped["k"] = interleave("wk", w_planes[K_COLS], "vector")
+        widen(w_planes[Q_COLS], Q_COLS, 0, "scalar")
+        widen(w_planes[Q_COLS], Q_COLS, 1, "scalar")
+        widen(w_planes[Q_COLS], Q_COLS, 2, "vector")
+        widen(w_planes[Q_COLS], Q_COLS, 3, "vector")
+        wk_q[0] = quantize("wk", w_grouped["k"])
+        w_grouped["q"] = interleave("wq", w_planes[Q_COLS], "vector")
+        relu_layer_passes(accs[0], turned[0], 0, 1)
+        relu(p_planes[0], 0, accs[0])
+        relu_layer_passes(accs[1], turned[0], 1, 1)
+        relu(p_planes[0], 1, accs[1])
+        relu_layer_passes(accs[2], turned[0], 2, 1)
+        relu(p_planes[0], 2, accs[2])
+        relu_layer_passes(accs[3], turned[0], 3, 1)
+        relu(p_planes[0], 3, accs[3])
+        B_["tp1"] = turn_prev(1)
+        B_["tc0"] = turn_cur(0)
+        wq_q[0] = quantize("wq", w_grouped["q"])
+        p_grouped[0] = interleave("p0", p_planes[0], "vector")
+        turned[1][0] = empty_prev(1, 0, B_["tp1"][0], "scalar")
+        turned[1][1] = empty_prev(1, 1, B_["tp1"][1], "scalar")
+        empty_cur(cur_grouped[0], 0, B_["tc0"][0], "scalar")
+        empty_cur(cur_grouped[0], 1, B_["tc0"][1], "scalar")
+        widen(w_planes[V_COLS], V_COLS, 0, "vector")
+        widen(w_planes[V_COLS], V_COLS, 1, "vector")
+        pq[0] = quantize("p0", p_grouped[0])
+        cq[0] = quantize("cur0", cur_grouped[0])
+        widen(w_planes[V_COLS], V_COLS, 2, "scalar")
+        widen(w_planes[V_COLS], V_COLS, 3, "scalar")
+        accs[4] = bank("relu1_0"); relu_layer_passes(accs[4], turned[1], 0, 0)
+        relu_layer_passes(accs[4], turned[1], 0, 1)
+        relu(p_planes[1], 0, accs[4])
+        w_grouped["v"] = interleave("wv", w_planes[V_COLS], "vector")
+        accs[5] = bank("relu1_1"); relu_layer_passes(accs[5], turned[1], 1, 0)
+        relu_layer_passes(accs[5], turned[1], 1, 1)
+        relu(p_planes[1], 1, accs[5])
+        accs[6] = bank("relu1_2"); relu_layer_passes(accs[6], turned[1], 2, 0)
+        relu_layer_passes(accs[6], turned[1], 2, 1)
+        relu(p_planes[1], 2, accs[6])
+        wv_q[0] = quantize("wv", w_grouped["v"])
+        accs[7] = bank("relu1_3"); relu_layer_passes(accs[7], turned[1], 3, 0)
+        relu_layer_passes(accs[7], turned[1], 3, 1)
+        relu(p_planes[1], 3, accs[7])
+        B_["p0"] = score_products(0, pq[0])
+        B_["tc1"] = turn_cur(1)
+        p_grouped[1] = interleave("p1", p_planes[1], "vector")
+        K_["p0"] = copy_keys(B_["p0"][0])
+        score(0, K_["p0"], B_["p0"][1], inv, score_prev)
+        empty_cur(cur_grouped[1], 0, B_["tc1"][0], "scalar")
+        empty_cur(cur_grouped[1], 1, B_["tc1"][1], "scalar")
+        pq[1] = quantize("p1", p_grouped[1])
+        B_["c0"] = score_products(0, cq[0])
+        K_["c0"] = copy_keys(B_["c0"][0])
+        score(0, K_["c0"], B_["c0"][1], -inv, minus_score_cur)
+        cq[1] = quantize("cur1", cur_grouped[1])
+        B_["p1"] = score_products(1, pq[0])
+        K_["p1"] = copy_keys(B_["p1"][0])
+        score(1, K_["p1"], B_["p1"][1], inv, score_prev)
+        gate(0)
+        B_["c1"] = score_products(1, cq[0])
+        K_["c1"] = copy_keys(B_["c1"][0])
+        score(1, K_["c1"], B_["c1"][1], -inv, minus_score_cur)
+        B_["v0"] = value_products(0)
+        K_["v0"] = scale_prev(0, B_["v0"][0])
+        mix(0, K_["v0"], B_["v0"][1])
+        B_["p2"] = score_products(2, pq[0])
+        K_["p2"] = copy_keys(B_["p2"][0])
+        score(2, K_["p2"], B_["p2"][1], inv, score_prev)
+        gate(1)
+        B_["c2"] = score_products(2, cq[0])
+        K_["c2"] = copy_keys(B_["c2"][0])
+        score(2, K_["c2"], B_["c2"][1], -inv, minus_score_cur)
+        B_["v1"] = value_products(1)
+        K_["v1"] = scale_prev(1, B_["v1"][0])
+        mix(1, K_["v1"], B_["v1"][1])
+        B_["p3"] = score_products(3, pq[0])
+        K_["p3"] = copy_keys(B_["p3"][0])
+        score(3, K_["p3"], B_["p3"][1], inv, score_prev)
+        gate(2)
+        B_["c3"] = score_products(3, cq[0])
+        K_["c3"] = copy_keys(B_["c3"][0])
+        score(3, K_["c3"], B_["c3"][1], -inv, minus_score_cur)
+        B_["v2"] = value_products(2)
+        K_["v2"] = scale_prev(2, B_["v2"][0])
+        mix(2, K_["v2"], B_["v2"][1])
+        B_["p4"] = score_products(4, pq[1])
+        K_["p4"] = copy_keys(B_["p4"][0])
+        score(4, K_["p4"], B_["p4"][1], inv, score_prev)
+        gate(3)
+        B_["c4"] = score_products(4, cq[1])
+        K_["c4"] = copy_keys(B_["c4"][0])
+        score(4, K_["c4"], B_["c4"][1], -inv, minus_score_cur)
+        B_["v3"] = value_products(3)
+        K_["v3"] = scale_prev(3, B_["v3"][0])
+        mix(3, K_["v3"], B_["v3"][1])
+        B_["p5"] = score_products(5, pq[1])
+        K_["p5"] = copy_keys(B_["p5"][0])
+        score(5, K_["p5"], B_["p5"][1], inv, score_prev)
+        gate(4)
+        B_["c5"] = score_products(5, cq[1])
+        K_["c5"] = copy_keys(B_["c5"][0])
+        score(5, K_["c5"], B_["c5"][1], -inv, minus_score_cur)
+        B_["v4"] = value_products(4)
+        K_["v4"] = scale_prev(4, B_["v4"][0])
+        mix(4, K_["v4"], B_["v4"][1])
+        B_["p6"] = score_products(6, pq[1])
+        K_["p6"] = copy_keys(B_["p6"][0])
+        score(6, K_["p6"], B_["p6"][1], inv, score_prev)
+        gate(5)
+        B_["c6"] = score_products(6, cq[1])
+        K_["c6"] = copy_keys(B_["c6"][0])
+        score(6, K_["c6"], B_["c6"][1], -inv, minus_score_cur)
+        B_["p7"] = score_products(7, pq[1])
+        K_["p7"] = copy_keys(B_["p7"][0])
+        score(7, K_["p7"], B_["p7"][1], inv, score_prev)
+        gate(6)
+        B_["c7"] = score_products(7, cq[1])
+        K_["c7"] = copy_keys(B_["c7"][0])
+        score(7, K_["c7"], B_["c7"][1], -inv, minus_score_cur)
+        B_["v5"] = value_products(5)
+        K_["v5"] = scale_prev(5, B_["v5"][0])
+        mix(5, K_["v5"], B_["v5"][1])
+        B_["v6"] = value_products(6)
+        K_["v6"] = scale_prev(6, B_["v6"][0])
+        mix(6, K_["v6"], B_["v6"][1])
+        gate(7)
+        B_["v7"] = value_products(7)
+        K_["v7"] = scale_prev(7, B_["v7"][0])
+        mix(7, K_["v7"], B_["v7"][1])

@@ -39,23 +39,31 @@ def tile_aitmadaptiveinfotransfer_kernel(tc, q_prev, wt, bt, q_cur, wvkq_bytes, 
             queue.dma_start(out=tile[:], in_=source)
             return tile
 
-        prev_rows = q_prev.rearrange("(h p r) d -> h p (r d)", h=2, r=PACK)
-        cur_rows = q_cur.rearrange("(h p r) d -> h p (r d)", h=2, r=PACK)
-        out_rows = out.rearrange("(h p r) n -> h r p n", h=2, r=PACK)
+        prev_rows = q_prev.rearrange("(g p r) d -> g p (r d)", g=4, r=2)
+        cur_rows = q_cur.rearrange("(h j p r) d -> h p j (r d)", h=2, j=2, r=2)
+        out_rows = out.rearrange("(g p r) n -> g r p n", g=4, r=2)
         wt_rows = wt.rearrange("(u p e) c -> u p (e c)", u=2, e=2)
         w_rows = wvkq_bytes.rearrange("(p t) n -> p t n", t=PACK)
 
         w_scale = load("w_scale", wvkq_scale.rearrange("(p t) o -> p (t o)", t=PACK), F32, nc.scalar)
         bias = load("bias", bt.rearrange("(p t) -> p t", t=PACK), BF16, nc.scalar)
-        prev0 = [load("prev0_%d" % i, prev_rows[0][:, 2 * D * i : 2 * D * (i + 1)], BF16) for i in range(2)]
-        wt_sb = [load("wt_0", wt_rows[0], BF16)]
-        w_bytes = {K_COLS: load("w_bytes_k", w_rows[:, :, D : 2 * D], U8)}
-        wt_sb.append(load("wt_1", wt_rows[1], BF16))
-        w_bytes[Q_COLS] = load("w_bytes_q", w_rows[:, :, 2 * D :], U8)
-        prev1 = load("prev1", prev_rows[1], BF16)
-        cur = [load("cur0", cur_rows[0], BF16)]
-        w_bytes[V_COLS] = load("w_bytes_v", w_rows[:, :, :D], U8)
-        cur.append(load("cur1", cur_rows[1], BF16))
+        def load_cur(h):
+            tile = keep.tile([P, 4 * D], BF16, name="cur%d" % h, align_bytes=64)
+            nc.sync.dma_start(out=tile[:].rearrange("p (j x) -> p j x", j=2), in_=cur_rows[h])
+            return tile
+
+        prev, wt_sb, w_bytes, cur = {}, {}, {}, {}
+        prev[0] = load("prev0", prev_rows[0], BF16)
+        prev[1] = load("prev1", prev_rows[1], BF16)
+        wt_sb[0] = load("wt_0", wt_rows[0], BF16)
+        w_bytes[K_COLS] = load("w_bytes_k", w_rows[:, :, D * K_COLS : D * (K_COLS + 1)], U8)
+        wt_sb[1] = load("wt_1", wt_rows[1], BF16)
+        w_bytes[Q_COLS] = load("w_bytes_q", w_rows[:, :, D * Q_COLS : D * (Q_COLS + 1)], U8)
+        prev[2] = load("prev2", prev_rows[2], BF16)
+        prev[3] = load("prev3", prev_rows[3], BF16)
+        w_bytes[V_COLS] = load("w_bytes_v", w_rows[:, :, D * V_COLS : D * (V_COLS + 1)], U8)
+        cur[0] = load_cur(0)
+        cur[1] = load_cur(1)
 
         identity = keep.tile([P, P], F32, name="identity")
         make_identity(nc, identity[:])
@@ -73,20 +81,17 @@ def tile_aitmadaptiveinfotransfer_kernel(tc, q_prev, wt, bt, q_cur, wvkq_bytes, 
             else:
                 nc.scalar.copy(out=dst, in_=src)
 
-        def prev_words(h, r):
-            if h == 0:
-                return prev0[r // 2][:].bitcast(F32)[:, 256 * (r % 2) : 256 * (r % 2 + 1)]
-            return prev1[:].bitcast(F32)[:, 256 * r : 256 * (r + 1)]
-
-        def turn_prev(h):
-            banks = [bank("prev_t_%d_%d" % (h, u)) for u in range(2)]
-            for r in range(PACK):
+        def turn_prev(g):
+            source = bank("prev_t_%d" % g)
+            words = prev[g][:].bitcast(F32)
+            for r in range(2):
                 for u in range(2):
-                    nc.tensor.transpose(banks[u][:, P * r : P * (r + 1)], prev_words(h, r)[:, P * u : P * (u + 1)], identity[:])
-            return banks
+                    at = 256 * u + P * r
+                    nc.tensor.transpose(source[:, at : at + P], words[:, 256 * r + P * u : 256 * r + P * (u + 1)], identity[:])
+            return source
 
-        def empty_prev(h, u, source, engine):
-            turned = keep.tile([P, HALF], F32, name="prev_turned_%d_%d" % (h, u))
+        def empty_prev(g, source, engine):
+            turned = keep.tile([P, HALF], F32, name="prev_turned_%d" % g)
             copy_words(engine, turned[:], source[:])
             return turned
 
@@ -106,21 +111,21 @@ def tile_aitmadaptiveinfotransfer_kernel(tc, q_prev, wt, bt, q_cur, wvkq_bytes, 
         def relu_layer_passes(acc, turned, t, u):
             for e in range(2):
                 nc.tensor.matmul(
-                    out=acc[:],
+                    out=acc[:, :256],
                     lhsT=wt_sb[u][:, C * e + t : C * (e + 1) : PACK],
-                    rhs=turned[u][:].bitcast(BF16)[:, e : 2 * HALF : 2],
+                    rhs=turned[:].bitcast(BF16)[:, HALF * u + e : HALF * (u + 1) : 2],
                     start=(u == 0 and e == 0),
                     stop=(u == 1 and e == 1),
                 )
 
         def relu(planes, t, acc):
-            nc.scalar.activation(out=planes[:, t, :], in_=acc[:], func=ACT.Relu, bias=bias[:, t : t + 1])
+            nc.scalar.activation(out=planes[:, t, :], in_=acc[:, :256], func=ACT.Relu, bias=bias[:, t : t + 1])
 
-        def new_planes(name):
-            return keep.tile([P, PACK, 512], BF16, name=name)
+        def new_planes(name, width):
+            return keep.tile([P, PACK, width], BF16, name=name)
 
-        def new_grouped(name):
-            return keep.tile([P, PACK * 512], BF16, name=name, align_bytes=64)
+        def new_grouped(name, width):
+            return keep.tile([P, PACK * width], BF16, name=name, align_bytes=64)
 
         def widen(planes, cols, t, engine):
             source = w_bytes[cols][:, t, :].bitcast(FP8)
@@ -130,7 +135,7 @@ def tile_aitmadaptiveinfotransfer_kernel(tc, q_prev, wt, bt, q_cur, wvkq_bytes, 
                 nc.scalar.activation(out=planes[:, t, :], in_=source, func=ACT.Copy, scale=w_scale[:, t : t + 1])
 
         def interleave(name, planes, engine):
-            grouped = new_grouped(name)
+            grouped = new_grouped(name, planes.shape[2])
             if engine == "vector":
                 nc.vector.tensor_copy(
                     out=grouped[:].rearrange("p (c i t) -> p c t i", i=4, t=PACK),
@@ -145,8 +150,9 @@ def tile_aitmadaptiveinfotransfer_kernel(tc, q_prev, wt, bt, q_cur, wvkq_bytes, 
             return grouped
 
         def quantize(name, grouped):
-            codes = keep.tile([P, 512], U32, name=name + "_codes", align_bytes=64)
-            scales = keep.tile([P, 512], U8, name=name + "_scales", align_bytes=64)
+            width = grouped.shape[1] // PACK
+            codes = keep.tile([P, width], U32, name=name + "_codes", align_bytes=64)
+            scales = keep.tile([P, width], U8, name=name + "_scales", align_bytes=64)
             nc.vector.quantize_mx(out=codes[:].bitcast(FP8X4), scales=scales[:], in_=grouped[:])
             return codes, scales
 
@@ -170,8 +176,8 @@ def tile_aitmadaptiveinfotransfer_kernel(tc, q_prev, wt, bt, q_cur, wvkq_bytes, 
             for what in ("score_prev", "minus_score_cur", "share_prev", "share_cur")
         )
 
-        def score_products(i, rows):
-            return product("k_%d" % i, rows, i % PACK, wk_q[0]), product("q_%d" % i, rows, i % PACK, wq_q[0])
+        def score_products(i, rows, r):
+            return product("k_%d" % i, rows, r, wk_q[0]), product("q_%d" % i, rows, r, wq_q[0])
 
         def copy_keys(keys_acc):
             keys = work.tile([P, D], F32, name="keys")
@@ -185,168 +191,212 @@ def tile_aitmadaptiveinfotransfer_kernel(tc, q_prev, wt, bt, q_cur, wvkq_bytes, 
 
         def gate(i):
             nc.scalar.activation(out=share_prev[i][:], in_=score_prev[i][:], func=ACT.Sigmoid, bias=minus_score_cur[i][:])
-            nc.gpsimd.tensor_scalar(out=share_cur[i][:], in0=share_prev[i][:], scalar1=-1.0, scalar2=1.0, op0=ALU.mult, op1=ALU.add)
+            (nc.vector if i == tiles - 1 else nc.gpsimd).tensor_scalar(out=share_cur[i][:], in0=share_prev[i][:], scalar1=-1.0, scalar2=1.0, op0=ALU.mult, op1=ALU.add)
 
         def value_products(i):
-            h, r = divmod(i, PACK)
-            return product("vp_%d" % i, pq[h], r, wv_q[0]), product("vc_%d" % i, cq[h], r, wv_q[0])
+            return product("vp_%d" % i, pq[i // 2], i % 2, wv_q[0]), product("vc_%d" % i, cq[i // 4], i % 4, wv_q[0])
 
-        def scale_prev(i, values_prev):
-            mixed = work.tile([P, D], F32, name="mixed")
-            nc.scalar.activation(out=mixed[:], in_=values_prev[:], func=ACT.Copy, scale=share_prev[i][:])
+        def scale_prev(i, values_prev, cols=slice(0, D)):
+            mixed = work.tile([P, cols.stop - cols.start], F32, name="mixed")
+            nc.scalar.activation(out=mixed[:], in_=values_prev[:, cols], func=ACT.Copy, scale=share_prev[i][:])
             return mixed
 
-        def mix(i, mixed, values_cur):
-            h, r = divmod(i, PACK)
+        def mix(i, mixed, values_cur, cols=slice(0, D)):
             nc.vector.scalar_tensor_tensor(
-                out=mixed[:], in0=values_cur[:], scalar=share_cur[i][:], in1=mixed[:], op0=ALU.mult, op1=ALU.add
+                out=mixed[:], in0=values_cur[:, cols], scalar=share_cur[i][:], in1=mixed[:], op0=ALU.mult, op1=ALU.add
             )
-            nc.sync.dma_start(out=out_rows[h][r], in_=mixed[:])
+            nc.sync.dma_start(out=out_rows[i // 2][i % 2][:, cols], in_=mixed[:])
 
         inv = 1.0 / math.sqrt(D)
-        turned = [{}, {}]
-        accs, p_grouped, w_grouped, pq, cq, B_, K_ = {}, {}, {}, {}, {}, {}, {}
+        turned = {}
+        accs, p_grouped, w_grouped, pq, cq, held, made = {}, {}, {}, {}, {}, {}, {}
         wk_q, wq_q, wv_q = {}, {}, {}
-        w_planes = [new_planes("w_planes_%d" % c) for c in range(3)]
-        p_planes = [new_planes("p_planes_%d" % h) for h in range(2)]
-        cur_grouped = [new_grouped("cur_grouped_%d" % h) for h in range(2)]
-        B_["tp0"] = turn_prev(0)
-        turned[0][0] = empty_prev(0, 0, B_["tp0"][0], "vector")
-        turned[0][1] = empty_prev(0, 1, B_["tp0"][1], "scalar")
-        accs[0] = bank("relu0_0"); relu_layer_passes(accs[0], turned[0], 0, 0)
-        accs[1] = bank("relu0_1"); relu_layer_passes(accs[1], turned[0], 1, 0)
-        accs[2] = bank("relu0_2"); relu_layer_passes(accs[2], turned[0], 2, 0)
-        accs[3] = bank("relu0_3"); relu_layer_passes(accs[3], turned[0], 3, 0)
+        w_planes = [new_planes("w_planes_%d" % c, 512) for c in range(3)]
+        p_planes = [new_planes("p_planes_%d" % g, 256) for g in range(4)]
+        cur_grouped = [new_grouped("cur_grouped_%d" % h, 512) for h in range(2)]
+        held["tp0"] = turn_prev(0)
+        held["tp1"] = turn_prev(1)
+        turned[0] = empty_prev(0, held["tp0"], "scalar")
+        turned[1] = empty_prev(1, held["tp1"], "vector")
+        accs[0, 0] = bank("relu0_0")
+        relu_layer_passes(accs[0, 0], turned[0], 0, 0)
+        accs[0, 1] = bank("relu0_1")
+        relu_layer_passes(accs[0, 1], turned[0], 1, 0)
+        accs[0, 2] = bank("relu0_2")
+        relu_layer_passes(accs[0, 2], turned[0], 2, 0)
+        accs[0, 3] = bank("relu0_3")
+        relu_layer_passes(accs[0, 3], turned[0], 3, 0)
         widen(w_planes[K_COLS], K_COLS, 0, "vector")
         widen(w_planes[K_COLS], K_COLS, 1, "vector")
         widen(w_planes[K_COLS], K_COLS, 2, "vector")
         widen(w_planes[K_COLS], K_COLS, 3, "scalar")
         w_grouped["k"] = interleave("wk", w_planes[K_COLS], "vector")
-        widen(w_planes[Q_COLS], Q_COLS, 0, "scalar")
+        relu_layer_passes(accs[0, 0], turned[0], 0, 1)
+        relu(p_planes[0], 0, accs[0, 0])
         widen(w_planes[Q_COLS], Q_COLS, 1, "scalar")
-        widen(w_planes[Q_COLS], Q_COLS, 2, "vector")
+        relu_layer_passes(accs[0, 1], turned[0], 1, 1)
+        relu(p_planes[0], 1, accs[0, 1])
+        widen(w_planes[Q_COLS], Q_COLS, 2, "scalar")
+        relu_layer_passes(accs[0, 2], turned[0], 2, 1)
+        relu(p_planes[0], 2, accs[0, 2])
+        relu_layer_passes(accs[0, 3], turned[0], 3, 1)
+        relu(p_planes[0], 3, accs[0, 3])
+        widen(w_planes[Q_COLS], Q_COLS, 0, "vector")
         widen(w_planes[Q_COLS], Q_COLS, 3, "vector")
         wk_q[0] = quantize("wk", w_grouped["k"])
+        accs[1, 0] = bank("relu1_0")
+        relu_layer_passes(accs[1, 0], turned[1], 0, 0)
+        relu_layer_passes(accs[1, 0], turned[1], 0, 1)
+        relu(p_planes[1], 0, accs[1, 0])
+        accs[1, 1] = bank("relu1_1")
+        relu_layer_passes(accs[1, 1], turned[1], 1, 0)
+        relu_layer_passes(accs[1, 1], turned[1], 1, 1)
+        relu(p_planes[1], 1, accs[1, 1])
+        held["tp2"] = turn_prev(2)
+        held["tp3"] = turn_prev(3)
+        turned[2] = empty_prev(2, held["tp2"], "scalar")
         w_grouped["q"] = interleave("wq", w_planes[Q_COLS], "vector")
-        relu_layer_passes(accs[0], turned[0], 0, 1)
-        relu(p_planes[0], 0, accs[0])
-        relu_layer_passes(accs[1], turned[0], 1, 1)
-        relu(p_planes[0], 1, accs[1])
-        relu_layer_passes(accs[2], turned[0], 2, 1)
-        relu(p_planes[0], 2, accs[2])
-        relu_layer_passes(accs[3], turned[0], 3, 1)
-        relu(p_planes[0], 3, accs[3])
-        B_["tp1"] = turn_prev(1)
-        B_["tc0"] = turn_cur(0)
-        wq_q[0] = quantize("wq", w_grouped["q"])
+        accs[1, 2] = bank("relu1_2")
+        relu_layer_passes(accs[1, 2], turned[1], 2, 0)
+        relu_layer_passes(accs[1, 2], turned[1], 2, 1)
+        relu(p_planes[1], 2, accs[1, 2])
+        turned[3] = empty_prev(3, held["tp3"], "scalar")
+        accs[1, 3] = bank("relu1_3")
+        relu_layer_passes(accs[1, 3], turned[1], 3, 0)
+        relu_layer_passes(accs[1, 3], turned[1], 3, 1)
+        relu(p_planes[1], 3, accs[1, 3])
         p_grouped[0] = interleave("p0", p_planes[0], "vector")
-        turned[1][0] = empty_prev(1, 0, B_["tp1"][0], "scalar")
-        turned[1][1] = empty_prev(1, 1, B_["tp1"][1], "scalar")
-        empty_cur(cur_grouped[0], 0, B_["tc0"][0], "scalar")
-        empty_cur(cur_grouped[0], 1, B_["tc0"][1], "scalar")
+        wq_q[0] = quantize("wq", w_grouped["q"])
         widen(w_planes[V_COLS], V_COLS, 0, "vector")
         widen(w_planes[V_COLS], V_COLS, 1, "vector")
-        pq[0] = quantize("p0", p_grouped[0])
-        cq[0] = quantize("cur0", cur_grouped[0])
         widen(w_planes[V_COLS], V_COLS, 2, "scalar")
-        widen(w_planes[V_COLS], V_COLS, 3, "scalar")
-        accs[4] = bank("relu1_0"); relu_layer_passes(accs[4], turned[1], 0, 0)
-        relu_layer_passes(accs[4], turned[1], 0, 1)
-        relu(p_planes[1], 0, accs[4])
-        w_grouped["v"] = interleave("wv", w_planes[V_COLS], "vector")
-        accs[5] = bank("relu1_1"); relu_layer_passes(accs[5], turned[1], 1, 0)
-        relu_layer_passes(accs[5], turned[1], 1, 1)
-        relu(p_planes[1], 1, accs[5])
-        accs[6] = bank("relu1_2"); relu_layer_passes(accs[6], turned[1], 2, 0)
-        relu_layer_passes(accs[6], turned[1], 2, 1)
-        relu(p_planes[1], 2, accs[6])
-        wv_q[0] = quantize("wv", w_grouped["v"])
-        accs[7] = bank("relu1_3"); relu_layer_passes(accs[7], turned[1], 3, 0)
-        relu_layer_passes(accs[7], turned[1], 3, 1)
-        relu(p_planes[1], 3, accs[7])
-        B_["p0"] = score_products(0, pq[0])
-        B_["tc1"] = turn_cur(1)
         p_grouped[1] = interleave("p1", p_planes[1], "vector")
-        K_["p0"] = copy_keys(B_["p0"][0])
-        score(0, K_["p0"], B_["p0"][1], inv, score_prev)
-        empty_cur(cur_grouped[1], 0, B_["tc1"][0], "scalar")
-        empty_cur(cur_grouped[1], 1, B_["tc1"][1], "scalar")
+        pq[0] = quantize("p0", p_grouped[0])
+        accs[2, 0] = bank("relu2_0")
+        relu_layer_passes(accs[2, 0], turned[2], 0, 0)
+        relu_layer_passes(accs[2, 0], turned[2], 0, 1)
+        relu(p_planes[2], 0, accs[2, 0])
+        widen(w_planes[V_COLS], V_COLS, 3, "scalar")
+        accs[2, 1] = bank("relu2_1")
+        relu_layer_passes(accs[2, 1], turned[2], 1, 0)
+        relu_layer_passes(accs[2, 1], turned[2], 1, 1)
+        relu(p_planes[2], 1, accs[2, 1])
+        accs[2, 2] = bank("relu2_2")
+        relu_layer_passes(accs[2, 2], turned[2], 2, 0)
+        relu_layer_passes(accs[2, 2], turned[2], 2, 1)
+        relu(p_planes[2], 2, accs[2, 2])
+        accs[2, 3] = bank("relu2_3")
+        relu_layer_passes(accs[2, 3], turned[2], 3, 0)
+        relu_layer_passes(accs[2, 3], turned[2], 3, 1)
+        relu(p_planes[2], 3, accs[2, 3])
+        w_grouped["v"] = interleave("wv", w_planes[V_COLS], "vector")
         pq[1] = quantize("p1", p_grouped[1])
-        B_["c0"] = score_products(0, cq[0])
-        K_["c0"] = copy_keys(B_["c0"][0])
-        score(0, K_["c0"], B_["c0"][1], -inv, minus_score_cur)
-        cq[1] = quantize("cur1", cur_grouped[1])
-        B_["p1"] = score_products(1, pq[0])
-        K_["p1"] = copy_keys(B_["p1"][0])
-        score(1, K_["p1"], B_["p1"][1], inv, score_prev)
+        accs[3, 0] = bank("relu3_0")
+        relu_layer_passes(accs[3, 0], turned[3], 0, 0)
+        relu_layer_passes(accs[3, 0], turned[3], 0, 1)
+        relu(p_planes[3], 0, accs[3, 0])
+        accs[3, 1] = bank("relu3_1")
+        relu_layer_passes(accs[3, 1], turned[3], 1, 0)
+        relu_layer_passes(accs[3, 1], turned[3], 1, 1)
+        relu(p_planes[3], 1, accs[3, 1])
+        p_grouped[2] = interleave("p2", p_planes[2], "vector")
+        wv_q[0] = quantize("wv", w_grouped["v"])
+        accs[3, 2] = bank("relu3_2")
+        relu_layer_passes(accs[3, 2], turned[3], 2, 0)
+        relu_layer_passes(accs[3, 2], turned[3], 2, 1)
+        relu(p_planes[3], 2, accs[3, 2])
+        accs[3, 3] = bank("relu3_3")
+        relu_layer_passes(accs[3, 3], turned[3], 3, 0)
+        relu_layer_passes(accs[3, 3], turned[3], 3, 1)
+        relu(p_planes[3], 3, accs[3, 3])
+        held["tc0"] = turn_cur(0)
+        p_grouped[3] = interleave("p3", p_planes[3], "vector")
+        pq[2] = quantize("p2", p_grouped[2])
+        empty_cur(cur_grouped[0], 0, held["tc0"][0], "scalar")
+        empty_cur(cur_grouped[0], 1, held["tc0"][1], "scalar")
+        pq[3] = quantize("p3", p_grouped[3])
+        cq[0] = quantize("cur0", cur_grouped[0])
+        held["p0"] = score_products(0, pq[0 // 2], 0 % 2)
+        made["p0"] = copy_keys(held["p0"][0])
+        score(0, made["p0"], held["p0"][1], inv, score_prev)
+        held["p1"] = score_products(1, pq[1 // 2], 1 % 2)
+        made["p1"] = copy_keys(held["p1"][0])
+        score(1, made["p1"], held["p1"][1], inv, score_prev)
+        held["p2"] = score_products(2, pq[2 // 2], 2 % 2)
+        made["p2"] = copy_keys(held["p2"][0])
+        score(2, made["p2"], held["p2"][1], inv, score_prev)
+        held["p3"] = score_products(3, pq[3 // 2], 3 % 2)
+        made["p3"] = copy_keys(held["p3"][0])
+        score(3, made["p3"], held["p3"][1], inv, score_prev)
+        held["c0"] = score_products(0, cq[0 // 4], 0 % 4)
+        made["c0"] = copy_keys(held["c0"][0])
+        score(0, made["c0"], held["c0"][1], -inv, minus_score_cur)
+        held["c1"] = score_products(1, cq[1 // 4], 1 % 4)
+        made["c1"] = copy_keys(held["c1"][0])
+        score(1, made["c1"], held["c1"][1], -inv, minus_score_cur)
+        held["tc1"] = turn_cur(1)
+        empty_cur(cur_grouped[1], 0, held["tc1"][0], "scalar")
+        empty_cur(cur_grouped[1], 1, held["tc1"][1], "scalar")
         gate(0)
-        B_["c1"] = score_products(1, cq[0])
-        K_["c1"] = copy_keys(B_["c1"][0])
-        score(1, K_["c1"], B_["c1"][1], -inv, minus_score_cur)
-        B_["v0"] = value_products(0)
-        K_["v0"] = scale_prev(0, B_["v0"][0])
-        mix(0, K_["v0"], B_["v0"][1])
-        B_["p2"] = score_products(2, pq[0])
-        K_["p2"] = copy_keys(B_["p2"][0])
-        score(2, K_["p2"], B_["p2"][1], inv, score_prev)
+        cq[1] = quantize("cur1", cur_grouped[1])
+        held["c2"] = score_products(2, cq[2 // 4], 2 % 4)
+        made["c2"] = copy_keys(held["c2"][0])
+        score(2, made["c2"], held["c2"][1], -inv, minus_score_cur)
+        held["v0"] = value_products(0)
+        made["v0"] = scale_prev(0, held["v0"][0])
+        mix(0, made["v0"], held["v0"][1])
         gate(1)
-        B_["c2"] = score_products(2, cq[0])
-        K_["c2"] = copy_keys(B_["c2"][0])
-        score(2, K_["c2"], B_["c2"][1], -inv, minus_score_cur)
-        B_["v1"] = value_products(1)
-        K_["v1"] = scale_prev(1, B_["v1"][0])
-        mix(1, K_["v1"], B_["v1"][1])
-        B_["p3"] = score_products(3, pq[0])
-        K_["p3"] = copy_keys(B_["p3"][0])
-        score(3, K_["p3"], B_["p3"][1], inv, score_prev)
+        held["c3"] = score_products(3, cq[3 // 4], 3 % 4)
+        made["c3"] = copy_keys(held["c3"][0])
+        score(3, made["c3"], held["c3"][1], -inv, minus_score_cur)
+        held["v1"] = value_products(1)
+        made["v1"] = scale_prev(1, held["v1"][0])
+        mix(1, made["v1"], held["v1"][1])
         gate(2)
-        B_["c3"] = score_products(3, cq[0])
-        K_["c3"] = copy_keys(B_["c3"][0])
-        score(3, K_["c3"], B_["c3"][1], -inv, minus_score_cur)
-        B_["v2"] = value_products(2)
-        K_["v2"] = scale_prev(2, B_["v2"][0])
-        mix(2, K_["v2"], B_["v2"][1])
-        B_["p4"] = score_products(4, pq[1])
-        K_["p4"] = copy_keys(B_["p4"][0])
-        score(4, K_["p4"], B_["p4"][1], inv, score_prev)
+        held["p4"] = score_products(4, pq[4 // 2], 4 % 2)
+        made["p4"] = copy_keys(held["p4"][0])
+        score(4, made["p4"], held["p4"][1], inv, score_prev)
+        held["v2"] = value_products(2)
+        made["v2"] = scale_prev(2, held["v2"][0])
+        mix(2, made["v2"], held["v2"][1])
         gate(3)
-        B_["c4"] = score_products(4, cq[1])
-        K_["c4"] = copy_keys(B_["c4"][0])
-        score(4, K_["c4"], B_["c4"][1], -inv, minus_score_cur)
-        B_["v3"] = value_products(3)
-        K_["v3"] = scale_prev(3, B_["v3"][0])
-        mix(3, K_["v3"], B_["v3"][1])
-        B_["p5"] = score_products(5, pq[1])
-        K_["p5"] = copy_keys(B_["p5"][0])
-        score(5, K_["p5"], B_["p5"][1], inv, score_prev)
+        held["c4"] = score_products(4, cq[4 // 4], 4 % 4)
+        made["c4"] = copy_keys(held["c4"][0])
+        score(4, made["c4"], held["c4"][1], -inv, minus_score_cur)
+        held["v3"] = value_products(3)
+        made["v3"] = scale_prev(3, held["v3"][0])
+        mix(3, made["v3"], held["v3"][1])
+        held["p5"] = score_products(5, pq[5 // 2], 5 % 2)
+        made["p5"] = copy_keys(held["p5"][0])
+        score(5, made["p5"], held["p5"][1], inv, score_prev)
         gate(4)
-        B_["c5"] = score_products(5, cq[1])
-        K_["c5"] = copy_keys(B_["c5"][0])
-        score(5, K_["c5"], B_["c5"][1], -inv, minus_score_cur)
-        B_["v4"] = value_products(4)
-        K_["v4"] = scale_prev(4, B_["v4"][0])
-        mix(4, K_["v4"], B_["v4"][1])
-        B_["p6"] = score_products(6, pq[1])
-        K_["p6"] = copy_keys(B_["p6"][0])
-        score(6, K_["p6"], B_["p6"][1], inv, score_prev)
+        held["c5"] = score_products(5, cq[5 // 4], 5 % 4)
+        made["c5"] = copy_keys(held["c5"][0])
+        score(5, made["c5"], held["c5"][1], -inv, minus_score_cur)
+        held["v4"] = value_products(4)
+        made["v4"] = scale_prev(4, held["v4"][0])
+        mix(4, made["v4"], held["v4"][1])
+        held["p6"] = score_products(6, pq[6 // 2], 6 % 2)
+        made["p6"] = copy_keys(held["p6"][0])
+        score(6, made["p6"], held["p6"][1], inv, score_prev)
         gate(5)
-        B_["c6"] = score_products(6, cq[1])
-        K_["c6"] = copy_keys(B_["c6"][0])
-        score(6, K_["c6"], B_["c6"][1], -inv, minus_score_cur)
-        B_["p7"] = score_products(7, pq[1])
-        K_["p7"] = copy_keys(B_["p7"][0])
-        score(7, K_["p7"], B_["p7"][1], inv, score_prev)
+        held["c6"] = score_products(6, cq[6 // 4], 6 % 4)
+        made["c6"] = copy_keys(held["c6"][0])
+        score(6, made["c6"], held["c6"][1], -inv, minus_score_cur)
+        held["v5"] = value_products(5)
+        made["v5"] = scale_prev(5, held["v5"][0])
+        mix(5, made["v5"], held["v5"][1])
+        held["p7"] = score_products(7, pq[7 // 2], 7 % 2)
+        made["p7"] = copy_keys(held["p7"][0])
+        score(7, made["p7"], held["p7"][1], inv, score_prev)
         gate(6)
-        B_["c7"] = score_products(7, cq[1])
-        K_["c7"] = copy_keys(B_["c7"][0])
-        score(7, K_["c7"], B_["c7"][1], -inv, minus_score_cur)
-        B_["v5"] = value_products(5)
-        K_["v5"] = scale_prev(5, B_["v5"][0])
-        mix(5, K_["v5"], B_["v5"][1])
-        B_["v6"] = value_products(6)
-        K_["v6"] = scale_prev(6, B_["v6"][0])
-        mix(6, K_["v6"], B_["v6"][1])
+        held["c7"] = score_products(7, cq[7 // 4], 7 % 4)
+        made["c7"] = copy_keys(held["c7"][0])
+        score(7, made["c7"], held["c7"][1], -inv, minus_score_cur)
+        held["v6"] = value_products(6)
+        made["v6"] = scale_prev(6, held["v6"][0])
+        mix(6, made["v6"], held["v6"][1])
         gate(7)
-        B_["v7"] = value_products(7)
-        K_["v7"] = scale_prev(7, B_["v7"][0])
-        mix(7, K_["v7"], B_["v7"][1])
+        held["v7"] = value_products(7)
+        for cols in (slice(0, D // 2), slice(D // 2, D)):
+            mix(7, scale_prev(7, held["v7"][0], cols), held["v7"][1], cols)

@@ -20,7 +20,6 @@ P = 128
 PACK = 4
 HALF = 512
 V_COLS, K_COLS, Q_COLS = 0, 1, 2
-WARM_UP_MATMULS = 6
 
 
 def tile_aitmadaptiveinfotransfer_kernel(tc, q_prev, wt, bt, q_cur, wvkq_bytes, wvkq_scale, out):
@@ -67,13 +66,10 @@ def tile_aitmadaptiveinfotransfer_kernel(tc, q_prev, wt, bt, q_cur, wvkq_bytes, 
 
         identity = keep.tile([P, P], F32, name="identity")
         make_identity(nc, identity[:])
-        zeros = keep.tile([P, 512], BF16, name="zeros")
+        zeros = keep.tile([P, 2], BF16, name="zeros")
         nc.vector.memset(zeros[:], 0.0)
         preload = keep.tile([P, 1], F32, name="preload")
         nc.scalar.activation(out=preload[:], in_=zeros[:, 0:1], func=ACT.Sigmoid)
-        warm = bank("warm")
-        for i in range(WARM_UP_MATMULS):
-            nc.tensor.matmul(out=warm[:], lhsT=zeros[:, :P], rhs=zeros[:], start=True, stop=True)
 
         def copy_words(engine, dst, src):
             if engine == "vector":

@@ -18,131 +18,140 @@ ALU = mybir.AluOpType
 
 P = 128
 PACK = 4
-HALF = 512
-V_COLS, K_COLS, Q_COLS = 0, 1, 2
+BANK = 512
+GROUP = 256
+WORDS = D // 2
+TILES = B // P
+HALF_TILES = TILES // 2
+V_PART, K_PART, Q_PART = 0, 1, 2
+PLANES_ON_VECTOR = {K_PART: 3, Q_PART: 2, V_PART: 2}
+WARM_UP_FIRST, WARM_UP_SECOND = 4, 2
+WORK_BUFS = 4
 
 
 def tile_aitmadaptiveinfotransfer_kernel(tc, q_prev, wt, bt, q_cur, wvkq_bytes, wvkq_scale, out):
     nc = tc.nc
     with ExitStack() as ctx:
         keep = ctx.enter_context(tc.tile_pool(name="keep", bufs=1))
-        work = ctx.enter_context(tc.tile_pool(name="work", bufs=4))
+        work = ctx.enter_context(tc.tile_pool(name="work", bufs=WORK_BUFS))
         psum = ctx.enter_context(tc.psum_pool(name="psum", bufs=8))
         ctx.enter_context(tc.manual_schedule())
 
         def bank(name):
-            return psum.tile([P, 512], F32, name=name, tag="bank")
+            return psum.tile([P, BANK], F32, name=name, tag="bank")
 
         def load(name, source, dtype, queue=nc.sync):
             tile = keep.tile(list(source.shape), dtype, name=name, align_bytes=64)
             queue.dma_start(out=tile[:], in_=source)
             return tile
 
-        prev_rows = q_prev.rearrange("(g p r) d -> g p (r d)", g=4, r=2)
-        cur_rows = q_cur.rearrange("(h j p r) d -> h p j (r d)", h=2, j=2, r=2)
-        out_rows = out.rearrange("(g p r) n -> g r p n", g=4, r=2)
-        wt_rows = wt.rearrange("(u p e) c -> u p (e c)", u=2, e=2)
-        w_rows = wvkq_bytes.rearrange("(p t) n -> p t n", t=PACK)
+        prev_rows = q_prev.rearrange("(g m r) d -> g m (r d)", m=P, r=2)
+        cur_rows = q_cur.rearrange("(h j m r) d -> h m j (r d)", j=2, m=P, r=2)
+        out_rows = out.rearrange("(g m r) n -> g r m n", m=P, r=2)
+        wt_rows = wt.rearrange("(u m e) c -> u m (e c)", m=P, e=2)
+        w_rows = wvkq_bytes.rearrange("(m t) n -> m t n", t=PACK)
 
-        w_scale = load("w_scale", wvkq_scale.rearrange("(p t) o -> p (t o)", t=PACK), F32, nc.scalar)
-        bias = load("bias", bt.rearrange("(p t) -> p t", t=PACK), BF16, nc.scalar)
+        def load_prev(g):
+            return load("prev%d" % g, prev_rows[g], BF16)
+
+        def load_wt(u):
+            return load("wt_%d" % u, wt_rows[u], BF16)
+
+        def load_bytes(part):
+            return load("w_bytes_%d" % part, w_rows[:, :, D * part : D * (part + 1)], U8)
+
         def load_cur(h):
-            tile = keep.tile([P, 4 * D], BF16, name="cur%d" % h, align_bytes=64)
-            nc.sync.dma_start(out=tile[:].rearrange("p (j x) -> p j x", j=2), in_=cur_rows[h])
+            tile = keep.tile([P, HALF_TILES * C], BF16, name="cur%d" % h, align_bytes=64)
+            nc.sync.dma_start(out=tile[:].rearrange("m (j x) -> m j x", j=2), in_=cur_rows[h])
             return tile
 
-        prev, wt_sb, w_bytes, cur = {}, {}, {}, {}
-        prev[0] = load("prev0", prev_rows[0], BF16)
-        prev[1] = load("prev1", prev_rows[1], BF16)
-        wt_sb[0] = load("wt_0", wt_rows[0], BF16)
-        w_bytes[K_COLS] = load("w_bytes_k", w_rows[:, :, D * K_COLS : D * (K_COLS + 1)], U8)
-        wt_sb[1] = load("wt_1", wt_rows[1], BF16)
-        w_bytes[Q_COLS] = load("w_bytes_q", w_rows[:, :, D * Q_COLS : D * (Q_COLS + 1)], U8)
-        prev[2] = load("prev2", prev_rows[2], BF16)
-        prev[3] = load("prev3", prev_rows[3], BF16)
-        w_bytes[V_COLS] = load("w_bytes_v", w_rows[:, :, D * V_COLS : D * (V_COLS + 1)], U8)
-        cur[0] = load_cur(0)
-        cur[1] = load_cur(1)
+        w_scale = load("w_scale", wvkq_scale.rearrange("(m t) o -> m (t o)", t=PACK), F32, nc.scalar)
+        bias = load("bias", bt.rearrange("(m t) -> m t", t=PACK), BF16, nc.scalar)
+        prev = [load_prev(0), load_prev(1)]
+        wt_sb = [load_wt(0)]
+        w_bytes = {K_PART: load_bytes(K_PART)}
+        wt_sb.append(load_wt(1))
+        w_bytes[Q_PART] = load_bytes(Q_PART)
+        prev.extend([load_prev(2), load_prev(3)])
+        w_bytes[V_PART] = load_bytes(V_PART)
+        cur = [load_cur(0), load_cur(1)]
 
         identity = keep.tile([P, P], F32, name="identity")
         make_identity(nc, identity[:])
-        zeros = keep.tile([P, 2], BF16, name="zeros")
-        nc.vector.memset(zeros[:], 0.0)
+        zeros = keep.tile([P, BANK], BF16, name="zeros")
+        nc.vector.memset(zeros[:].bitcast(U32), 0)
         preload = keep.tile([P, 1], F32, name="preload")
         nc.scalar.activation(out=preload[:], in_=zeros[:, 0:1], func=ACT.Sigmoid)
+        warm = bank("warm")
 
-        def copy_words(engine, dst, src):
-            if engine == "vector":
-                nc.vector.tensor_copy(out=dst, in_=src)
-            else:
-                nc.scalar.copy(out=dst, in_=src)
+        def warm_up(count):
+            for i in range(count):
+                nc.tensor.matmul(out=warm[:], lhsT=zeros[:, :P], rhs=zeros[:], start=True, stop=True)
 
         def turn_prev(g):
-            source = bank("prev_t_%d" % g)
+            turned = bank("prev_t_%d" % g)
             words = prev[g][:].bitcast(F32)
             for r in range(2):
                 for u in range(2):
-                    at = 256 * u + P * r
-                    nc.tensor.transpose(source[:, at : at + P], words[:, 256 * r + P * u : 256 * r + P * (u + 1)], identity[:])
-            return source
-
-        def empty_prev(g, source, engine):
-            turned = keep.tile([P, HALF], F32, name="prev_turned_%d" % g)
-            copy_words(engine, turned[:], source[:])
+                    at = GROUP * u + P * r
+                    nc.tensor.transpose(turned[:, at : at + P], words[:, WORDS * r + P * u : WORDS * r + P * (u + 1)], identity[:])
             return turned
 
-        def turn_cur(h):
-            banks = [bank("cur_t_%d_%d" % (h, j)) for j in range(2)]
-            words = cur[h][:].bitcast(F32)
-            for r in range(PACK):
-                for u in range(2):
-                    at = 256 * (r % 2) + P * u
-                    nc.tensor.transpose(banks[r // 2][:, at : at + P], words[:, 256 * r + u : 256 * (r + 1) : 2], identity[:])
-            return banks
+        def empty_prev(g, turned, copy):
+            moving = keep.tile([P, BANK], F32, name="prev_turned_%d" % g)
+            copy(out=moving[:], in_=turned[:])
+            return moving
 
-        def empty_cur(grouped, j, source, engine):
-            dst = grouped[:].bitcast(F32)[:, HALF * j : HALF * (j + 1)]
-            copy_words(engine, dst.rearrange("p (r m u) -> p r m u", r=2, u=2), source[:].rearrange("p (r u m) -> p r m u", r=2, u=2))
-
-        def relu_layer_passes(acc, turned, t, u):
+        def relu_passes(acc, moving, t, u):
             for e in range(2):
                 nc.tensor.matmul(
-                    out=acc[:, :256],
+                    out=acc[:, :GROUP],
                     lhsT=wt_sb[u][:, C * e + t : C * (e + 1) : PACK],
-                    rhs=turned[:].bitcast(BF16)[:, HALF * u + e : HALF * (u + 1) : 2],
+                    rhs=moving[:].bitcast(BF16)[:, 2 * GROUP * u + e : 2 * GROUP * (u + 1) : 2],
                     start=(u == 0 and e == 0),
                     stop=(u == 1 and e == 1),
                 )
 
-        def relu(planes, t, acc):
-            nc.scalar.activation(out=planes[:, t, :], in_=acc[:, :256], func=ACT.Relu, bias=bias[:, t : t + 1])
+        def relu(g, t, acc):
+            nc.scalar.activation(out=p_planes[g][:, t, :], in_=acc[:, :GROUP], func=ACT.Relu, bias=bias[:, t : t + 1])
 
-        def new_planes(name, width):
-            return keep.tile([P, PACK, width], BF16, name=name)
+        def relu_plane(g, t, moving):
+            acc = bank("relu%d_%d" % (g, t))
+            for u in range(2):
+                relu_passes(acc, moving, t, u)
+            relu(g, t, acc)
 
-        def new_grouped(name, width):
-            return keep.tile([P, PACK * width], BF16, name=name, align_bytes=64)
+        def turn_cur(h):
+            banks = [bank("cur_t_%d_%d" % (h, j)) for j in range(2)]
+            words = cur[h][:].bitcast(F32)
+            for i in range(HALF_TILES):
+                for u in range(2):
+                    at = GROUP * (i % 2) + P * u
+                    nc.tensor.transpose(banks[i // 2][:, at : at + P], words[:, WORDS * i + u : WORDS * (i + 1) : 2], identity[:])
+            return banks
 
-        def widen(planes, cols, t, engine):
-            source = w_bytes[cols][:, t, :].bitcast(FP8)
-            if engine == "vector":
-                nc.vector.tensor_scalar(out=planes[:, t, :], in0=source, scalar1=w_scale[:, t : t + 1], scalar2=None, op0=ALU.mult)
-            else:
-                nc.scalar.activation(out=planes[:, t, :], in_=source, func=ACT.Copy, scale=w_scale[:, t : t + 1])
-
-        def interleave(name, planes, engine):
-            grouped = new_grouped(name, planes.shape[2])
-            if engine == "vector":
-                nc.vector.tensor_copy(
-                    out=grouped[:].rearrange("p (c i t) -> p c t i", i=4, t=PACK),
-                    in_=planes[:].rearrange("p t (c i) -> p c t i", i=4),
+        def empty_cur(h, banks):
+            for j in range(2):
+                dst = cur_grouped[h][:].bitcast(F32)[:, BANK * j : BANK * (j + 1)]
+                nc.scalar.copy(
+                    out=dst.rearrange("m (r x u) -> m r x u", r=2, u=2),
+                    in_=banks[j][:].rearrange("m (r u x) -> m r x u", r=2, u=2),
                 )
+
+        def widen(part, t):
+            source = w_bytes[part][:, t, :].bitcast(FP8)
+            plane = w_planes[part][:, t, :]
+            if t < PLANES_ON_VECTOR[part]:
+                nc.vector.tensor_scalar(out=plane, in0=source, scalar1=w_scale[:, t : t + 1], scalar2=None, op0=ALU.mult)
             else:
-                nc.gpsimd.tensor_scalar(
-                    out=grouped[:].rearrange("p (c t) -> p c t", t=PACK),
-                    in0=planes[:].rearrange("p t c -> p c t"),
-                    scalar1=1.0, scalar2=0.0, op0=ALU.mult, op1=ALU.add,
-                )
+                nc.scalar.activation(out=plane, in_=source, func=ACT.Copy, scale=w_scale[:, t : t + 1])
+
+        def interleave(name, planes):
+            grouped = keep.tile([P, PACK * planes.shape[2]], BF16, name=name, align_bytes=64)
+            nc.vector.tensor_copy(
+                out=grouped[:].rearrange("m (c i t) -> m c t i", i=4, t=PACK),
+                in_=planes[:].rearrange("m t (c i) -> m c t i", i=4),
+            )
             return grouped
 
         def quantize(name, grouped):
@@ -152,247 +161,140 @@ def tile_aitmadaptiveinfotransfer_kernel(tc, q_prev, wt, bt, q_cur, wvkq_bytes, 
             nc.vector.quantize_mx(out=codes[:].bitcast(FP8X4), scales=scales[:], in_=grouped[:])
             return codes, scales
 
-        def product(name, rows, r, weights):
+        def product(name, rows, part):
             acc = bank(name)
-            cols = slice(P * r, P * (r + 1))
+            codes, scales = w_mx[part]
             nc.tensor.matmul_mx(
                 out=acc[:],
-                lhsT=rows[0][:, cols].bitcast(FP8X4),
-                lhsT_scale=rows[1][:, cols],
-                rhs=weights[0][:].bitcast(FP8X4),
-                rhs_scale=weights[1][:],
+                lhsT=rows[0].bitcast(FP8X4),
+                lhsT_scale=rows[1],
+                rhs=codes[:].bitcast(FP8X4),
+                rhs_scale=scales[:],
                 start=True,
                 stop=True,
             )
             return acc
 
-        tiles = 2 * PACK
-        score_prev, minus_score_cur, share_prev, share_cur = (
-            [keep.tile([P, 1], F32, name="%s_%d" % (what, i)) for i in range(tiles)]
-            for what in ("score_prev", "minus_score_cur", "share_prev", "share_cur")
-        )
+        def row_tile(quantized, i):
+            per_entry = quantized[0][0].shape[1] // P
+            codes, scales = quantized[i // per_entry]
+            cols = slice(P * (i % per_entry), P * (i % per_entry + 1))
+            return codes[:, cols], scales[:, cols]
 
-        def score_products(i, rows, r):
-            return product("k_%d" % i, rows, r, wk_q[0]), product("q_%d" % i, rows, r, wq_q[0])
-
-        def copy_keys(keys_acc):
+        def score(i, quantized, factor, result):
+            rows = row_tile(quantized, i)
+            keys_acc = product("k_%d" % i, rows, K_PART)
+            queries = product("q_%d" % i, rows, Q_PART)
             keys = work.tile([P, D], F32, name="keys")
             nc.scalar.copy(out=keys[:], in_=keys_acc[:])
-            return keys
-
-        def score(i, keys, queries, factor, result):
             nc.vector.scalar_tensor_tensor(
-                out=keys[:], in0=queries[:], scalar=factor, in1=keys[:], op0=ALU.mult, op1=ALU.mult, accum_out=result[i][:]
+                out=keys[:], in0=queries[:], scalar=factor, in1=keys[:], op0=ALU.mult, op1=ALU.mult, accum_out=result[:]
             )
+
+        def score_prev(i):
+            score(i, p_mx, 1.0 / math.sqrt(D), sp[i])
+
+        def score_cur(i):
+            score(i, cur_mx, -1.0 / math.sqrt(D), minus_sc[i])
 
         def gate(i):
-            nc.scalar.activation(out=share_prev[i][:], in_=score_prev[i][:], func=ACT.Sigmoid, bias=minus_score_cur[i][:])
-            (nc.vector if i == tiles - 1 else nc.gpsimd).tensor_scalar(out=share_cur[i][:], in0=share_prev[i][:], scalar1=-1.0, scalar2=1.0, op0=ALU.mult, op1=ALU.add)
+            nc.scalar.activation(out=share_prev[i][:], in_=sp[i][:], func=ACT.Sigmoid, bias=minus_sc[i][:])
+            engine = nc.vector if i == TILES - 1 else nc.gpsimd
+            engine.tensor_scalar(out=share_cur[i][:], in0=share_prev[i][:], scalar1=-1.0, scalar2=1.0, op0=ALU.mult, op1=ALU.add)
 
-        def value_products(i):
-            return product("vp_%d" % i, pq[i // 2], i % 2, wv_q[0]), product("vc_%d" % i, cq[i // 4], i % 4, wv_q[0])
+        def mix(i, pieces=1):
+            values_prev = product("vp_%d" % i, row_tile(p_mx, i), V_PART)
+            values_cur = product("vc_%d" % i, row_tile(cur_mx, i), V_PART)
+            width = D // pieces
+            for at in range(0, D, width):
+                cols = slice(at, at + width)
+                mixed = work.tile([P, width], F32, name="mixed")
+                nc.scalar.activation(out=mixed[:], in_=values_prev[:, cols], func=ACT.Copy, scale=share_prev[i][:])
+                nc.vector.scalar_tensor_tensor(
+                    out=mixed[:], in0=values_cur[:, cols], scalar=share_cur[i][:], in1=mixed[:], op0=ALU.mult, op1=ALU.add
+                )
+                nc.sync.dma_start(out=out_rows[i // 2][i % 2][:, cols], in_=mixed[:])
 
-        def scale_prev(i, values_prev, cols=slice(0, D)):
-            mixed = work.tile([P, cols.stop - cols.start], F32, name="mixed")
-            nc.scalar.activation(out=mixed[:], in_=values_prev[:, cols], func=ACT.Copy, scale=share_prev[i][:])
-            return mixed
+        sp, minus_sc, share_prev, share_cur = (
+            [keep.tile([P, 1], F32, name="%s_%d" % (what, i)) for i in range(TILES)]
+            for what in ("sp", "minus_sc", "share_prev", "share_cur")
+        )
+        w_planes = [keep.tile([P, PACK, D], BF16, name="w_planes_%d" % part) for part in range(3)]
+        p_planes = [keep.tile([P, PACK, GROUP], BF16, name="p_planes_%d" % g) for g in range(B // GROUP)]
+        cur_grouped = [keep.tile([P, PACK * HALF_TILES * P], BF16, name="cur_grouped_%d" % h, align_bytes=64) for h in range(2)]
+        w_mx, p_mx, cur_mx = {}, [], []
 
-        def mix(i, mixed, values_cur, cols=slice(0, D)):
-            nc.vector.scalar_tensor_tensor(
-                out=mixed[:], in0=values_cur[:, cols], scalar=share_cur[i][:], in1=mixed[:], op0=ALU.mult, op1=ALU.add
-            )
-            nc.sync.dma_start(out=out_rows[i // 2][i % 2][:, cols], in_=mixed[:])
+        warm_up(WARM_UP_FIRST)
+        turned = [turn_prev(0), turn_prev(1)]
+        warm_up(WARM_UP_SECOND)
+        moving = [empty_prev(0, turned[0], nc.scalar.copy), empty_prev(1, turned[1], nc.vector.tensor_copy)]
 
-        inv = 1.0 / math.sqrt(D)
-        turned = {}
-        accs, p_grouped, w_grouped, pq, cq, held, made = {}, {}, {}, {}, {}, {}, {}
-        wk_q, wq_q, wv_q = {}, {}, {}
-        w_planes = [new_planes("w_planes_%d" % c, 512) for c in range(3)]
-        p_planes = [new_planes("p_planes_%d" % g, 256) for g in range(4)]
-        cur_grouped = [new_grouped("cur_grouped_%d" % h, 512) for h in range(2)]
-        held["tp0"] = turn_prev(0)
-        held["tp1"] = turn_prev(1)
-        turned[0] = empty_prev(0, held["tp0"], "scalar")
-        turned[1] = empty_prev(1, held["tp1"], "vector")
-        accs[0, 0] = bank("relu0_0")
-        relu_layer_passes(accs[0, 0], turned[0], 0, 0)
-        accs[0, 1] = bank("relu0_1")
-        relu_layer_passes(accs[0, 1], turned[0], 1, 0)
-        accs[0, 2] = bank("relu0_2")
-        relu_layer_passes(accs[0, 2], turned[0], 2, 0)
-        accs[0, 3] = bank("relu0_3")
-        relu_layer_passes(accs[0, 3], turned[0], 3, 0)
-        widen(w_planes[K_COLS], K_COLS, 0, "vector")
-        widen(w_planes[K_COLS], K_COLS, 1, "vector")
-        widen(w_planes[K_COLS], K_COLS, 2, "vector")
-        widen(w_planes[K_COLS], K_COLS, 3, "scalar")
-        w_grouped["k"] = interleave("wk", w_planes[K_COLS], "vector")
-        relu_layer_passes(accs[0, 0], turned[0], 0, 1)
-        relu(p_planes[0], 0, accs[0, 0])
-        widen(w_planes[Q_COLS], Q_COLS, 1, "scalar")
-        relu_layer_passes(accs[0, 1], turned[0], 1, 1)
-        relu(p_planes[0], 1, accs[0, 1])
-        widen(w_planes[Q_COLS], Q_COLS, 2, "scalar")
-        relu_layer_passes(accs[0, 2], turned[0], 2, 1)
-        relu(p_planes[0], 2, accs[0, 2])
-        relu_layer_passes(accs[0, 3], turned[0], 3, 1)
-        relu(p_planes[0], 3, accs[0, 3])
-        widen(w_planes[Q_COLS], Q_COLS, 0, "vector")
-        widen(w_planes[Q_COLS], Q_COLS, 3, "vector")
-        wk_q[0] = quantize("wk", w_grouped["k"])
-        accs[1, 0] = bank("relu1_0")
-        relu_layer_passes(accs[1, 0], turned[1], 0, 0)
-        relu_layer_passes(accs[1, 0], turned[1], 0, 1)
-        relu(p_planes[1], 0, accs[1, 0])
-        accs[1, 1] = bank("relu1_1")
-        relu_layer_passes(accs[1, 1], turned[1], 1, 0)
-        relu_layer_passes(accs[1, 1], turned[1], 1, 1)
-        relu(p_planes[1], 1, accs[1, 1])
-        held["tp2"] = turn_prev(2)
-        held["tp3"] = turn_prev(3)
-        turned[2] = empty_prev(2, held["tp2"], "scalar")
-        w_grouped["q"] = interleave("wq", w_planes[Q_COLS], "vector")
-        accs[1, 2] = bank("relu1_2")
-        relu_layer_passes(accs[1, 2], turned[1], 2, 0)
-        relu_layer_passes(accs[1, 2], turned[1], 2, 1)
-        relu(p_planes[1], 2, accs[1, 2])
-        turned[3] = empty_prev(3, held["tp3"], "scalar")
-        accs[1, 3] = bank("relu1_3")
-        relu_layer_passes(accs[1, 3], turned[1], 3, 0)
-        relu_layer_passes(accs[1, 3], turned[1], 3, 1)
-        relu(p_planes[1], 3, accs[1, 3])
-        p_grouped[0] = interleave("p0", p_planes[0], "vector")
-        wq_q[0] = quantize("wq", w_grouped["q"])
-        widen(w_planes[V_COLS], V_COLS, 0, "vector")
-        widen(w_planes[V_COLS], V_COLS, 1, "vector")
-        widen(w_planes[V_COLS], V_COLS, 2, "scalar")
-        p_grouped[1] = interleave("p1", p_planes[1], "vector")
-        pq[0] = quantize("p0", p_grouped[0])
-        accs[2, 0] = bank("relu2_0")
-        relu_layer_passes(accs[2, 0], turned[2], 0, 0)
-        relu_layer_passes(accs[2, 0], turned[2], 0, 1)
-        relu(p_planes[2], 0, accs[2, 0])
-        widen(w_planes[V_COLS], V_COLS, 3, "scalar")
-        accs[2, 1] = bank("relu2_1")
-        relu_layer_passes(accs[2, 1], turned[2], 1, 0)
-        relu_layer_passes(accs[2, 1], turned[2], 1, 1)
-        relu(p_planes[2], 1, accs[2, 1])
-        accs[2, 2] = bank("relu2_2")
-        relu_layer_passes(accs[2, 2], turned[2], 2, 0)
-        relu_layer_passes(accs[2, 2], turned[2], 2, 1)
-        relu(p_planes[2], 2, accs[2, 2])
-        accs[2, 3] = bank("relu2_3")
-        relu_layer_passes(accs[2, 3], turned[2], 3, 0)
-        relu_layer_passes(accs[2, 3], turned[2], 3, 1)
-        relu(p_planes[2], 3, accs[2, 3])
-        w_grouped["v"] = interleave("wv", w_planes[V_COLS], "vector")
-        pq[1] = quantize("p1", p_grouped[1])
-        accs[3, 0] = bank("relu3_0")
-        relu_layer_passes(accs[3, 0], turned[3], 0, 0)
-        relu_layer_passes(accs[3, 0], turned[3], 0, 1)
-        relu(p_planes[3], 0, accs[3, 0])
-        accs[3, 1] = bank("relu3_1")
-        relu_layer_passes(accs[3, 1], turned[3], 1, 0)
-        relu_layer_passes(accs[3, 1], turned[3], 1, 1)
-        relu(p_planes[3], 1, accs[3, 1])
-        p_grouped[2] = interleave("p2", p_planes[2], "vector")
-        wv_q[0] = quantize("wv", w_grouped["v"])
-        accs[3, 2] = bank("relu3_2")
-        relu_layer_passes(accs[3, 2], turned[3], 2, 0)
-        relu_layer_passes(accs[3, 2], turned[3], 2, 1)
-        relu(p_planes[3], 2, accs[3, 2])
-        accs[3, 3] = bank("relu3_3")
-        relu_layer_passes(accs[3, 3], turned[3], 3, 0)
-        relu_layer_passes(accs[3, 3], turned[3], 3, 1)
-        relu(p_planes[3], 3, accs[3, 3])
-        held["tc0"] = turn_cur(0)
-        p_grouped[3] = interleave("p3", p_planes[3], "vector")
-        pq[2] = quantize("p2", p_grouped[2])
-        empty_cur(cur_grouped[0], 0, held["tc0"][0], "scalar")
-        empty_cur(cur_grouped[0], 1, held["tc0"][1], "scalar")
-        pq[3] = quantize("p3", p_grouped[3])
-        cq[0] = quantize("cur0", cur_grouped[0])
-        held["p0"] = score_products(0, pq[0 // 2], 0 % 2)
-        made["p0"] = copy_keys(held["p0"][0])
-        score(0, made["p0"], held["p0"][1], inv, score_prev)
-        held["p1"] = score_products(1, pq[1 // 2], 1 % 2)
-        made["p1"] = copy_keys(held["p1"][0])
-        score(1, made["p1"], held["p1"][1], inv, score_prev)
-        held["p2"] = score_products(2, pq[2 // 2], 2 % 2)
-        made["p2"] = copy_keys(held["p2"][0])
-        score(2, made["p2"], held["p2"][1], inv, score_prev)
-        held["p3"] = score_products(3, pq[3 // 2], 3 % 2)
-        made["p3"] = copy_keys(held["p3"][0])
-        score(3, made["p3"], held["p3"][1], inv, score_prev)
-        held["c0"] = score_products(0, cq[0 // 4], 0 % 4)
-        made["c0"] = copy_keys(held["c0"][0])
-        score(0, made["c0"], held["c0"][1], -inv, minus_score_cur)
-        held["c1"] = score_products(1, cq[1 // 4], 1 % 4)
-        made["c1"] = copy_keys(held["c1"][0])
-        score(1, made["c1"], held["c1"][1], -inv, minus_score_cur)
-        held["tc1"] = turn_cur(1)
-        empty_cur(cur_grouped[1], 0, held["tc1"][0], "scalar")
-        empty_cur(cur_grouped[1], 1, held["tc1"][1], "scalar")
+        accs = [bank("relu0_%d" % t) for t in range(PACK)]
+        for t in range(PACK):
+            relu_passes(accs[t], moving[0], t, 0)
+        for t in range(PACK):
+            widen(K_PART, t)
+        wk_grouped = interleave("wk", w_planes[K_PART])
+        widen(Q_PART, 0)
+        widen(Q_PART, 1)
+        for t in range(PACK):
+            relu_passes(accs[t], moving[0], t, 1)
+            relu(0, t, accs[t])
+            if t < 2:
+                widen(Q_PART, 2 + t)
+        w_mx[K_PART] = quantize("wk", wk_grouped)
+        wq_grouped = interleave("wq", w_planes[Q_PART])
+        p_grouped = [interleave("p0", p_planes[0])]
+        w_mx[Q_PART] = quantize("wq", wq_grouped)
+
+        relu_plane(1, 0, moving[1])
+        relu_plane(1, 1, moving[1])
+        turned = [turn_prev(2), turn_prev(3)]
+        for j in range(2):
+            moving.append(empty_prev(2 + j, turned[j], nc.scalar.copy))
+            relu_plane(1, 2 + j, moving[1])
+        for t in range(PACK - 1):
+            widen(V_PART, t)
+        p_grouped.append(interleave("p1", p_planes[1]))
+        p_mx.append(quantize("p0", p_grouped[0]))
+
+        relu_plane(2, 0, moving[2])
+        widen(V_PART, PACK - 1)
+        for t in range(1, PACK):
+            relu_plane(2, t, moving[2])
+        wv_grouped = interleave("wv", w_planes[V_PART])
+        p_mx.append(quantize("p1", p_grouped[1]))
+        p_grouped.append(interleave("p2", p_planes[2]))
+        w_mx[V_PART] = quantize("wv", wv_grouped)
+
+        for t in range(PACK):
+            relu_plane(3, t, moving[3])
+        cur_banks = turn_cur(0)
+        p_grouped.append(interleave("p3", p_planes[3]))
+        p_mx.append(quantize("p2", p_grouped[2]))
+        p_mx.append(quantize("p3", p_grouped[3]))
+        empty_cur(0, cur_banks)
+        cur_mx.append(quantize("cur0", cur_grouped[0]))
+
+        for i in range(HALF_TILES):
+            score_prev(i)
+        score_cur(0)
+        score_cur(1)
+        empty_cur(1, turn_cur(1))
         gate(0)
-        cq[1] = quantize("cur1", cur_grouped[1])
-        held["c2"] = score_products(2, cq[2 // 4], 2 % 4)
-        made["c2"] = copy_keys(held["c2"][0])
-        score(2, made["c2"], held["c2"][1], -inv, minus_score_cur)
-        held["v0"] = value_products(0)
-        made["v0"] = scale_prev(0, held["v0"][0])
-        mix(0, made["v0"], held["v0"][1])
-        gate(1)
-        held["c3"] = score_products(3, cq[3 // 4], 3 % 4)
-        made["c3"] = copy_keys(held["c3"][0])
-        score(3, made["c3"], held["c3"][1], -inv, minus_score_cur)
-        held["v1"] = value_products(1)
-        made["v1"] = scale_prev(1, held["v1"][0])
-        mix(1, made["v1"], held["v1"][1])
-        gate(2)
-        held["p4"] = score_products(4, pq[4 // 2], 4 % 2)
-        made["p4"] = copy_keys(held["p4"][0])
-        score(4, made["p4"], held["p4"][1], inv, score_prev)
-        held["v2"] = value_products(2)
-        made["v2"] = scale_prev(2, held["v2"][0])
-        mix(2, made["v2"], held["v2"][1])
-        gate(3)
-        held["c4"] = score_products(4, cq[4 // 4], 4 % 4)
-        made["c4"] = copy_keys(held["c4"][0])
-        score(4, made["c4"], held["c4"][1], -inv, minus_score_cur)
-        held["v3"] = value_products(3)
-        made["v3"] = scale_prev(3, held["v3"][0])
-        mix(3, made["v3"], held["v3"][1])
-        held["p5"] = score_products(5, pq[5 // 2], 5 % 2)
-        made["p5"] = copy_keys(held["p5"][0])
-        score(5, made["p5"], held["p5"][1], inv, score_prev)
-        gate(4)
-        held["c5"] = score_products(5, cq[5 // 4], 5 % 4)
-        made["c5"] = copy_keys(held["c5"][0])
-        score(5, made["c5"], held["c5"][1], -inv, minus_score_cur)
-        held["v4"] = value_products(4)
-        made["v4"] = scale_prev(4, held["v4"][0])
-        mix(4, made["v4"], held["v4"][1])
-        held["p6"] = score_products(6, pq[6 // 2], 6 % 2)
-        made["p6"] = copy_keys(held["p6"][0])
-        score(6, made["p6"], held["p6"][1], inv, score_prev)
-        gate(5)
-        held["c6"] = score_products(6, cq[6 // 4], 6 % 4)
-        made["c6"] = copy_keys(held["c6"][0])
-        score(6, made["c6"], held["c6"][1], -inv, minus_score_cur)
-        held["v5"] = value_products(5)
-        made["v5"] = scale_prev(5, held["v5"][0])
-        mix(5, made["v5"], held["v5"][1])
-        held["p7"] = score_products(7, pq[7 // 2], 7 % 2)
-        made["p7"] = copy_keys(held["p7"][0])
-        score(7, made["p7"], held["p7"][1], inv, score_prev)
-        gate(6)
-        held["c7"] = score_products(7, cq[7 // 4], 7 % 4)
-        made["c7"] = copy_keys(held["c7"][0])
-        score(7, made["c7"], held["c7"][1], -inv, minus_score_cur)
-        held["v6"] = value_products(6)
-        made["v6"] = scale_prev(6, held["v6"][0])
-        mix(6, made["v6"], held["v6"][1])
-        gate(7)
-        held["v7"] = value_products(7)
-        for cols in (slice(0, D // 2), slice(D // 2, D)):
-            mix(7, scale_prev(7, held["v7"][0], cols), held["v7"][1], cols)
+        cur_mx.append(quantize("cur1", cur_grouped[1]))
+        for i in range(2, HALF_TILES):
+            score_cur(i)
+            mix(i - 2)
+            gate(i - 1)
+        score_prev(HALF_TILES)
+        mix(HALF_TILES - 2)
+
+        for i in range(HALF_TILES, TILES):
+            gate(i - 1)
+            score_cur(i)
+            mix(i - 1)
+            if i + 1 < TILES:
+                score_prev(i + 1)
+        gate(TILES - 1)
+        mix(TILES - 1, pieces=2)

@@ -181,26 +181,31 @@ def tile_aitmadaptiveinfotransfer_kernel(tc, q_prev, wt, bt, q_cur, wvkq_bytes, 
             cols = slice(P * (i % per_entry), P * (i % per_entry + 1))
             return codes[:, cols], scales[:, cols]
 
-        def score(i, quantized, factor, result):
+        def score(i, quantized, result):
             rows = row_tile(quantized, i)
             keys_acc = product("k_%d" % i, rows, K_PART)
             queries = product("q_%d" % i, rows, Q_PART)
             keys = work.tile([P, D], F32, name="keys")
             nc.scalar.copy(out=keys[:], in_=keys_acc[:])
             nc.vector.scalar_tensor_tensor(
-                out=keys[:], in0=queries[:], scalar=factor, in1=keys[:], op0=ALU.mult, op1=ALU.mult, accum_out=result[:]
+                out=keys[:],
+                in0=queries[:],
+                scalar=1.0 / math.sqrt(D),
+                in1=keys[:],
+                op0=ALU.mult,
+                op1=ALU.mult,
+                accum_out=result[:],
             )
 
         def score_prev(i):
-            score(i, p_mx, 1.0 / math.sqrt(D), sp[i])
+            score(i, p_mx, sp[i])
 
         def score_cur(i):
-            score(i, cur_mx, -1.0 / math.sqrt(D), minus_sc[i])
+            score(i, cur_mx, sc[i])
 
         def gate(i):
-            nc.scalar.activation(out=share_prev[i][:], in_=sp[i][:], func=ACT.Sigmoid, bias=minus_sc[i][:])
-            engine = nc.vector if i == TILES - 1 else nc.gpsimd
-            engine.tensor_scalar(out=share_cur[i][:], in0=share_prev[i][:], scalar1=-1.0, scalar2=1.0, op0=ALU.mult, op1=ALU.add)
+            nc.scalar.activation(out=share_prev[i][:], in_=sc[i][:], func=ACT.Sigmoid, scale=-1.0, bias=sp[i][:])
+            nc.scalar.activation(out=share_cur[i][:], in_=sp[i][:], func=ACT.Sigmoid, scale=-1.0, bias=sc[i][:])
 
         def mix(i, pieces=1):
             values_prev = product("vp_%d" % i, row_tile(p_mx, i), V_PART)
@@ -215,9 +220,9 @@ def tile_aitmadaptiveinfotransfer_kernel(tc, q_prev, wt, bt, q_cur, wvkq_bytes, 
                 )
                 nc.sync.dma_start(out=out_rows[i // 2][i % 2][:, cols], in_=mixed[:])
 
-        sp, minus_sc, share_prev, share_cur = (
+        sp, sc, share_prev, share_cur = (
             [keep.tile([P, 1], F32, name="%s_%d" % (what, i)) for i in range(TILES)]
-            for what in ("sp", "minus_sc", "share_prev", "share_cur")
+            for what in ("sp", "sc", "share_prev", "share_cur")
         )
         w_planes = [keep.tile([P, PACK, D], BF16, name="w_planes_%d" % part) for part in range(3)]
         p_planes = [keep.tile([P, PACK, GROUP], BF16, name="p_planes_%d" % g) for g in range(B // GROUP)]

import math
from contextlib import ExitStack

import concourse.mybir as mybir
from concourse.masks import make_identity

B, D, C = 1024, 512, 512
FLOPS = 2 * B * D * C + 2 * 2 * B * C * 3 * D

F32 = mybir.dt.float32
BF16 = mybir.dt.bfloat16
U32 = mybir.dt.uint32
U8 = mybir.dt.uint8
FP8 = mybir.dt.float8_e4m3fn
FP8X4 = mybir.dt.float8_e4m3fn_x4
ACT = mybir.ActivationFunctionType
ALU = mybir.AluOpType

P = 128
PACK = 4
BANK = 512
GROUP = 256
WORDS = D // 2
TILES = B // P
HALF_TILES = TILES // 2
V_PART, K_PART, Q_PART = 0, 1, 2
PLANES_ON_VECTOR = {K_PART: 3, Q_PART: 2, V_PART: 2}
WARM_UP_FIRST, WARM_UP_SECOND = 4, 2
WORK_BUFS = 4


def tile_aitmadaptiveinfotransfer_kernel(tc, q_prev, wt, bt, q_cur, wvkq_bytes, wvkq_scale, out):
    nc = tc.nc
    with ExitStack() as ctx:
        keep = ctx.enter_context(tc.tile_pool(name="keep", bufs=1))
        work = ctx.enter_context(tc.tile_pool(name="work", bufs=WORK_BUFS))
        psum = ctx.enter_context(tc.psum_pool(name="psum", bufs=8))
        ctx.enter_context(tc.manual_schedule())

        def bank(name):
            return psum.tile([P, BANK], F32, name=name, tag="bank")

        def load(name, source, dtype, queue=nc.sync):
            tile = keep.tile(list(source.shape), dtype, name=name, align_bytes=64)
            queue.dma_start(out=tile[:], in_=source)
            return tile

        prev_rows = q_prev.rearrange("(g m r) d -> g m (r d)", m=P, r=2)
        cur_rows = q_cur.rearrange("(h j m r) d -> h m j (r d)", j=2, m=P, r=2)
        out_rows = out.rearrange("(g m r) n -> g r m n", m=P, r=2)
        wt_rows = wt.rearrange("(u m e) c -> u m (e c)", m=P, e=2)
        w_rows = wvkq_bytes.rearrange("(m t) n -> m t n", t=PACK)

        def load_prev(g):
            return load("prev%d" % g, prev_rows[g], BF16)

        def load_wt(u):
            return load("wt_%d" % u, wt_rows[u], BF16)

        def load_bytes(part):
            return load("w_bytes_%d" % part, w_rows[:, :, D * part : D * (part + 1)], U8)

        def load_cur(h):
            tile = keep.tile([P, HALF_TILES * C], BF16, name="cur%d" % h, align_bytes=64)
            nc.sync.dma_start(out=tile[:].rearrange("m (j x) -> m j x", j=2), in_=cur_rows[h])
            return tile

        w_scale = load("w_scale", wvkq_scale.rearrange("(m t) o -> m (t o)", t=PACK), F32, nc.scalar)
        bias = load("bias", bt.rearrange("(m t) -> m t", t=PACK), BF16, nc.scalar)
        prev = [load_prev(0), load_prev(1)]
        wt_sb = [load_wt(0)]
        w_bytes = {K_PART: load_bytes(K_PART)}
        wt_sb.append(load_wt(1))
        w_bytes[Q_PART] = load_bytes(Q_PART)
        prev.extend([load_prev(2), load_prev(3)])
        w_bytes[V_PART] = load_bytes(V_PART)
        cur = [load_cur(0), load_cur(1)]

        identity = keep.tile([P, P], F32, name="identity")
        make_identity(nc, identity[:])
        zeros = keep.tile([P, BANK], BF16, name="zeros")
        nc.vector.memset(zeros[:].bitcast(U32), 0)
        preload = keep.tile([P, 1], F32, name="preload")
        nc.scalar.activation(out=preload[:], in_=zeros[:, 0:1], func=ACT.Sigmoid)
        warm = bank("warm")

        def warm_up(count):
            for i in range(count):
                nc.tensor.matmul(out=warm[:], lhsT=zeros[:, :P], rhs=zeros[:], start=True, stop=True)

        def turn_prev(g):
            turned = bank("prev_t_%d" % g)
            words = prev[g][:].bitcast(F32)
            for r in range(2):
                for u in range(2):
                    at = GROUP * u + P * r
                    nc.tensor.transpose(turned[:, at : at + P], words[:, WORDS * r + P * u : WORDS * r + P * (u + 1)], identity[:])
            return turned

        def empty_prev(g, turned, copy):
            moving = keep.tile([P, BANK], F32, name="prev_turned_%d" % g)
            copy(out=moving[:], in_=turned[:])
            return moving

        def relu_passes(acc, moving, t, u):
            for e in range(2):
                nc.tensor.matmul(
                    out=acc[:, :GROUP],
                    lhsT=wt_sb[u][:, C * e + t : C * (e + 1) : PACK],
                    rhs=moving[:].bitcast(BF16)[:, 2 * GROUP * u + e : 2 * GROUP * (u + 1) : 2],
                    start=(u == 0 and e == 0),
                    stop=(u == 1 and e == 1),
                )

        def relu(g, t, acc):
            nc.scalar.activation(out=p_planes[g][:, t, :], in_=acc[:, :GROUP], func=ACT.Relu, bias=bias[:, t : t + 1])

        def relu_plane(g, t, moving):
            acc = bank("relu%d_%d" % (g, t))
            for u in range(2):
                relu_passes(acc, moving, t, u)
            relu(g, t, acc)

        def turn_cur(h):
            banks = [bank("cur_t_%d_%d" % (h, j)) for j in range(2)]
            words = cur[h][:].bitcast(F32)
            for i in range(HALF_TILES):
                for u in range(2):
                    at = GROUP * (i % 2) + P * u
                    nc.tensor.transpose(banks[i // 2][:, at : at + P], words[:, WORDS * i + u : WORDS * (i + 1) : 2], identity[:])
            return banks

        def empty_cur(h, banks):
            for j in range(2):
                dst = cur_grouped[h][:].bitcast(F32)[:, BANK * j : BANK * (j + 1)]
                nc.scalar.copy(
                    out=dst.rearrange("m (r x u) -> m r x u", r=2, u=2),
                    in_=banks[j][:].rearrange("m (r u x) -> m r x u", r=2, u=2),
                )

        def widen(part, t):
            source = w_bytes[part][:, t, :].bitcast(FP8)
            plane = w_planes[part][:, t, :]
            if t < PLANES_ON_VECTOR[part]:
                nc.vector.tensor_scalar(out=plane, in0=source, scalar1=w_scale[:, t : t + 1], scalar2=None, op0=ALU.mult)
            else:
                nc.scalar.activation(out=plane, in_=source, func=ACT.Copy, scale=w_scale[:, t : t + 1])

        def interleave(name, planes):
            grouped = keep.tile([P, PACK * planes.shape[2]], BF16, name=name, align_bytes=64)
            nc.vector.tensor_copy(
                out=grouped[:].rearrange("m (c i t) -> m c t i", i=4, t=PACK),
                in_=planes[:].rearrange("m t (c i) -> m c t i", i=4),
            )
            return grouped

        def quantize(name, grouped):
            width = grouped.shape[1] // PACK
            codes = keep.tile([P, width], U32, name=name + "_codes", align_bytes=64)
            scales = keep.tile([P, width], U8, name=name + "_scales", align_bytes=64)
            nc.vector.quantize_mx(out=codes[:].bitcast(FP8X4), scales=scales[:], in_=grouped[:])
            return codes, scales

        def product(name, rows, part):
            acc = bank(name)
            codes, scales = w_mx[part]
            nc.tensor.matmul_mx(
                out=acc[:],
                lhsT=rows[0].bitcast(FP8X4),
                lhsT_scale=rows[1],
                rhs=codes[:].bitcast(FP8X4),
                rhs_scale=scales[:],
                start=True,
                stop=True,
            )
            return acc

        def row_tile(quantized, i):
            per_entry = quantized[0][0].shape[1] // P
            codes, scales = quantized[i // per_entry]
            cols = slice(P * (i % per_entry), P * (i % per_entry + 1))
            return codes[:, cols], scales[:, cols]

        def score(i, quantized, result):
            rows = row_tile(quantized, i)
            keys_acc = product("k_%d" % i, rows, K_PART)
            queries = product("q_%d" % i, rows, Q_PART)
            keys = work.tile([P, D], F32, name="keys")
            nc.scalar.copy(out=keys[:], in_=keys_acc[:])
            nc.vector.scalar_tensor_tensor(
                out=keys[:],
                in0=queries[:],
                scalar=1.0 / math.sqrt(D),
                in1=keys[:],
                op0=ALU.mult,
                op1=ALU.mult,
                accum_out=result[:],
            )

        def score_prev(i):
            score(i, p_mx, sp[i])

        def score_cur(i):
            score(i, cur_mx, sc[i])

        def gate(i):
            nc.scalar.activation(out=share_prev[i][:], in_=sc[i][:], func=ACT.Sigmoid, scale=-1.0, bias=sp[i][:])
            nc.scalar.activation(out=share_cur[i][:], in_=sp[i][:], func=ACT.Sigmoid, scale=-1.0, bias=sc[i][:])

        def mix(i, pieces=1):
            values_prev = product("vp_%d" % i, row_tile(p_mx, i), V_PART)
            values_cur = product("vc_%d" % i, row_tile(cur_mx, i), V_PART)
            width = D // pieces
            for at in range(0, D, width):
                cols = slice(at, at + width)
                mixed = work.tile([P, width], F32, name="mixed")
                nc.scalar.activation(out=mixed[:], in_=values_prev[:, cols], func=ACT.Copy, scale=share_prev[i][:])
                nc.vector.scalar_tensor_tensor(
                    out=mixed[:], in0=values_cur[:, cols], scalar=share_cur[i][:], in1=mixed[:], op0=ALU.mult, op1=ALU.add
                )
                nc.sync.dma_start(out=out_rows[i // 2][i % 2][:, cols], in_=mixed[:])

        sp, sc, share_prev, share_cur = (
            [keep.tile([P, 1], F32, name="%s_%d" % (what, i)) for i in range(TILES)]
            for what in ("sp", "sc", "share_prev", "share_cur")
        )
        w_planes = [keep.tile([P, PACK, D], BF16, name="w_planes_%d" % part) for part in range(3)]
        p_planes = [keep.tile([P, PACK, GROUP], BF16, name="p_planes_%d" % g) for g in range(B // GROUP)]
        cur_grouped = [keep.tile([P, PACK * HALF_TILES * P], BF16, name="cur_grouped_%d" % h, align_bytes=64) for h in range(2)]
        w_mx, p_mx, cur_mx = {}, [], []

        warm_up(WARM_UP_FIRST)
        turned = [turn_prev(0), turn_prev(1)]
        warm_up(WARM_UP_SECOND)
        moving = [empty_prev(0, turned[0], nc.scalar.copy), empty_prev(1, turned[1], nc.vector.tensor_copy)]

        accs = [bank("relu0_%d" % t) for t in range(PACK)]
        for t in range(PACK):
            relu_passes(accs[t], moving[0], t, 0)
        for t in range(PACK):
            widen(K_PART, t)
        wk_grouped = interleave("wk", w_planes[K_PART])
        widen(Q_PART, 0)
        widen(Q_PART, 1)
        for t in range(PACK):
            relu_passes(accs[t], moving[0], t, 1)
            relu(0, t, accs[t])
            if t < 2:
                widen(Q_PART, 2 + t)
        w_mx[K_PART] = quantize("wk", wk_grouped)
        wq_grouped = interleave("wq", w_planes[Q_PART])
        p_grouped = [interleave("p0", p_planes[0])]
        w_mx[Q_PART] = quantize("wq", wq_grouped)

        relu_plane(1, 0, moving[1])
        relu_plane(1, 1, moving[1])
        turned = [turn_prev(2), turn_prev(3)]
        for j in range(2):
            moving.append(empty_prev(2 + j, turned[j], nc.scalar.copy))
            relu_plane(1, 2 + j, moving[1])
        for t in range(PACK - 1):
            widen(V_PART, t)
        p_grouped.append(interleave("p1", p_planes[1]))
        p_mx.append(quantize("p0", p_grouped[0]))

        relu_plane(2, 0, moving[2])
        widen(V_PART, PACK - 1)
        for t in range(1, PACK):
            relu_plane(2, t, moving[2])
        wv_grouped = interleave("wv", w_planes[V_PART])
        p_mx.append(quantize("p1", p_grouped[1]))
        p_grouped.append(interleave("p2", p_planes[2]))
        w_mx[V_PART] = quantize("wv", wv_grouped)

        for t in range(PACK):
            relu_plane(3, t, moving[3])
        cur_banks = turn_cur(0)
        p_grouped.append(interleave("p3", p_planes[3]))
        p_mx.append(quantize("p2", p_grouped[2]))
        p_mx.append(quantize("p3", p_grouped[3]))
        empty_cur(0, cur_banks)
        cur_mx.append(quantize("cur0", cur_grouped[0]))

        for i in range(HALF_TILES):
            score_prev(i)
        score_cur(0)
        score_cur(1)
        empty_cur(1, turn_cur(1))
        gate(0)
        cur_mx.append(quantize("cur1", cur_grouped[1]))
        for i in range(2, HALF_TILES):
            score_cur(i)
            mix(i - 2)
            gate(i - 1)
        score_prev(HALF_TILES)
        mix(HALF_TILES - 2)

        for i in range(HALF_TILES, TILES):
            gate(i - 1)
            score_cur(i)
            mix(i - 1)
            if i + 1 < TILES:
                score_prev(i + 1)
        gate(TILES - 1)
        mix(TILES - 1, pieces=2)
